import numpy as np, ml_dtypes
CORES = [113,118,241,246]
N = 4
BF = ml_dtypes.bfloat16
W, E, S, M, RO, DB, DC, CM, EX = 1536, 192, 8, 6, 4, 2, 1, 9, 6
def pack(x, p, r, z):
    return {"x0": np.ascontiguousarray(x.reshape(N, 128, W)).astype(np.float32).astype(BF), "lk": np.ascontiguousarray(p.reshape(N, 128, W)).astype(np.int32),
            "rd": np.ascontiguousarray(r.reshape(N, 128, E)).astype(np.int32), "z0": np.ascontiguousarray(z.reshape(N, 128, E)).astype(np.float32).astype(BF)}
def parts(rng):
    lev = np.repeat(rng.choice(np.array([24, 60, 120, 190, 255]), (N, 8, 1, 8)), W // 8, axis=3)
    x = (rng.random((N, 8, 16, W)) * (lev + 1)).astype(np.int64) * (rng.random((N, 8, 1, W)) > 0.0625)
    share = np.stack([rng.permutation(np.array([0.1, 0.1, 0.3, 0.3, 0.6, 0.6, 0.9, 0.95])) for q in range(N)]).reshape(N, 8, 1, 1)
    to = np.where(rng.random((N, 8, 16, W)) < 0.5, S * rng.integers(0, E, (N, 8, 16, W)), rng.integers(0, W, (N, 8, 16, W)))
    p = np.where(rng.random((N, 8, 16, W)) < share, to, W)
    near = rng.integers(0, 8, (N, 8, 1, E)) * (W // 8) + rng.integers(0, W // 8, (N, 8, 16, E))
    r = np.where(rng.random((N, 8, 1, E)) < 0.5, near, rng.integers(0, W, (N, 8, 16, E)))
    z = (rng.random((N, 8, 16, E)) * (rng.choice(np.array([40, 120, 255]), (N, 8, 1, E)) + 1)).astype(np.int64)
    return x, p, r, z
def setup_inputs(rng):
    return pack(*parts(rng))
def setup_inputs_spread(rng):
    x = np.minimum((np.exp2(9 * rng.random((N, 8, 1, W))) * rng.random((N, 8, 16, W))).astype(np.int64), 255)
    z = np.minimum((np.exp2(9 * rng.random((N, 8, 1, E))) * rng.random((N, 8, 16, E))).astype(np.int64), 255)
    to = np.minimum((W * rng.random((N, 8, 16, W)) ** 3).astype(np.int64), W - 1)
    p = np.where(rng.random((N, 8, 16, W)) < rng.random((N, 8, 16, 1)), to, W)
    r = np.minimum((W * rng.random((N, 8, 16, E)) ** rng.choice(np.array([1.0, 2.0, 4.0]), (N, 8, 1, 1))).astype(np.int64), W - 1)
    return pack(x, p, r, z)
def setup_inputs_ends(rng):
    kind = rng.integers(0, 4, (N, 8, 1, W)); el = 255 * rng.integers(0, 2, (N, 8, 16, W))
    x = np.where(kind == 0, 0, np.where(kind == 1, 255, el))
    v = rng.permutation(np.array([0, 255] * 4)); x[..., 0] = v[None, :, None]; x[..., W - 1] = 255 - v[None, :, None]
    x[..., W - 2] = 255 - v[None, :, None]; x[:, :, 15, W - 2] = np.where(v == 0, 254, 1)[None, :]
    p = np.where(rng.random((N, 8, 16, W)) < 0.2, rng.integers(0, W, (N, 8, 16, W)), W * (rng.random((N, 8, 16, W)) < 0.65))
    p[..., 0] = W; p[:, :, 0, 0] = W - 2; p[:, :, [1, 15], 0] = W - 1; p[..., W - 1] = W; p[:, :, [0, 15], W - 1] = 0
    way = rng.integers(0, 4, (N, 8, 1, E)); way[..., 0] = 0; way[..., E - 2] = 0; way[..., E - 1] = 1
    end = (W - 1) * rng.integers(0, 2, (N, 8, 16, E)); some = np.where(rng.random((N, 8, 16, E)) < 0.5, end, rng.integers(0, W, (N, 8, 16, E)))
    r = np.where(way == 0, 0, np.where(way == 1, W - 1, np.where(way == 2, end, some)))
    z = 255 * np.where(rng.random((N, 8, 1, E)) < 0.5, rng.integers(0, 2, (N, 8, 1, E)), rng.integers(0, 2, (N, 8, 16, E)))
    return pack(x, p, r, z)
def setup_inputs_corners(rng):
    x, p, r, z = parts(rng); gt = rng.permutation(8); H = W // 2
    for g in range(8):
        m = int(gt[g])
        if m < 2:
            x[:, g, :, 1::2] = 128
            h = rng.integers(0, 17, (N, 1, H)) if m == 0 else rng.choice(np.array([EX, EX + 1, CM - 1, CM]), (N, 1, H))
            up = np.argsort(rng.random((N, 16, H)), axis=1) < h; one = rng.random((N, 16, H)) < (0.5 if m == 0 else 2.0)
            x[:, g, :, 0::2] = np.where(up, np.where(one, 128, rng.integers(128, 256, (N, 16, H))), np.where(one, 127, rng.integers(0, 128, (N, 16, H))))
            p[:, g] = np.where(rng.random((N, 16, W)) < 0.4, 2 * rng.integers(0, H, (N, 16, W)), W)
            r[:, g] = 2 * rng.integers(0, H, (N, 16, E)) + 1
        elif m == 2:
            full = rng.integers(0, W, (N, 16, W)); p[:, g] = np.where((np.arange(N) % 2 == 0)[:, None, None], full, W)
        elif m == 3:
            r[:, g] = S * np.arange(E)[None, :] + (np.arange(16) % S)[:, None]
            p[:, g] = np.where(rng.random((N, 16, W)) < 0.5, S * (np.arange(W) // S), W)
            x[:, g, :, 0::S] = x[:, g, :, 0::S] * (rng.random((N, 1, E)) < 0.5)
        elif m == 4:
            x[:, g] = x[:, g] * (rng.random((N, 1, W)) < 0.3); z[:, g] = z[:, g] * (rng.random((N, 1, E)) < 0.5)
            x[:, g, :15, 0::S] = 0; x[:, g, 15, 0::S] = rng.integers(1, 256, (N, E)) * (rng.random((N, E)) < 0.5)
            p[:, g] = np.where(rng.random((N, 16, W)) < 0.5, rng.integers(0, W, (N, 16, W)), W)
        elif m == 5:
            p[:, g] = rng.choice(np.array([0, W - 1, W]), (N, 16, W))
            r[:, g] = np.where(rng.random((N, 16, E)) < 0.5, (W - 1) * rng.integers(0, 2, (N, 16, E)), r[:, g])
        elif m == 6:
            p[:, g] = np.where(rng.random((N, 16, W)) < 0.5, rng.integers(0, W, (N, 16, W)), W)
            x[:, g, :, 0::S] = np.maximum(x[:, g, :, 0::S], 1)
            for b in range(N):
                a = S * rng.permutation(E) + 1; d = S * rng.permutation(E) + S - 1
                high = rng.integers(128, 256, (16, E)); low = rng.integers(1, 100, (16, E))
                x[b, g][:, a] = high if b % 2 == 0 else low
                x[(b + DC) % N, g][:, d] = low if b % 2 == 0 else high
                up = np.argsort(rng.random((16, E)), axis=0) < rng.integers(1, 16, (1, E))
                p[b, g][:, a] = np.where(up, d[None, :], W)
                r[(b - DB) % N, g] = a[None, :]
        else:
            p[:, g] = W; p[:, g, 0] = S * rng.integers(0, E, (N, W)); p[:, g, 15] = rng.integers(0, W, (N, W))
    return pack(x, p, r, z)
def setup_inputs_crowd(rng):
    x, p, r, z = parts(rng); gt = rng.permutation(8)
    for g in range(8):
        m = int(gt[g]); i = int(rng.integers(1, E - 1)); b = S * i + (0 if m in (0, 3, 5, 6) else S - 1)
        a = (0, W - 1, S * (i - 1) + 1, S * i + 1)[m % 4]
        x[:, g, :, a] = rng.integers(128, 256, (N, 16)); x[:, g, :, b] = rng.integers(1, 100, (N, 16))
        p[:, g, :, a] = W; rows = rng.permutation(16)[:5]; p[:, g, rows, a] = b
        r[:, g] = a
        if m >= 4: r[:, g, :, (0, E - 1, 1, i)[m % 4]] = rng.integers(0, W, (N, 16))
    return pack(x, p, r, z)
def check_inputs(d):
    bad = []
    for k, lo, hi in (("x0", 0, 255), ("lk", 0, W), ("rd", 0, W - 1), ("z0", 0, 255)):
        v = np.asarray(d[k]).astype(np.float64)
        if not (np.min(v) >= lo and np.max(v) <= hi): bad.append("range of " + k)
        if np.any(v != np.floor(v)): bad.append("whole numbers of " + k)
        if np.any((v == 0) & np.signbit(v)): bad.append("-0.0 in " + k)
    return bad
def reference(x0, lk, rd, z0):
    X = x0.astype(np.float32).astype(np.int64).reshape(N, 8, 16, W); P = lk.astype(np.int64).reshape(N, 8, 16, W)
    R = rd.astype(np.int64).reshape(N, 8, 16, E); z = z0.astype(np.float32).astype(np.int64).reshape(N, 8, 16, E)
    bi = (np.arange(N) + DB) % N; ci = (np.arange(N) + DB + DC) % N; lane = np.arange(E)
    q = np.zeros((N, 8, E), np.int64) + S * lane
    rows = np.arange(16)[None, None, :, None]; ai = np.arange(N)[:, None, None]; gi = np.arange(8)[None, :, None]
    for t in range(RO):
        XB = X[bi]; PB = P[bi]; flat = R.reshape(N, 8, 1, 16 * E)
        L = np.take_along_axis(PB, R, 3)
        xs = np.take_along_axis(XB, flat, 3).reshape(N, 8, 16, 16, E)
        free = (L == W)[:, :, None]
        top = np.max(np.where(free, xs, -1), axis=3); low = np.min(np.where(free, xs, 256), axis=3)
        y = np.where(top >= 0, (top + low) >> 1, z)
        XC = X[ci]
        orphan = ~np.any(np.take_along_axis(XC, q[:, :, None, :], 3) != 0, axis=2)
        q = np.where(orphan, S * lane + (y[:, :, 0] & 7), q)
        np.put_along_axis(XC, q[:, :, None, :], y, 3)
        es = np.take_along_axis(XC, np.minimum(L, W - 1).reshape(N, 8, 1, 16 * E), 3).reshape(N, 8, 16, 16, E)
        yk = y[:, :, :, None, :]
        n = np.add.reduce((es >= yk).astype(np.int64), axis=2); dist = np.add.reduce(np.abs(es - yk), axis=2)
        com = (L < W) & (n >= CM); late = (L < W) & (n <= EX); settled = com | late
        ks = np.where(np.any(settled, axis=2), np.argmax(np.where(settled, dist, -1), axis=2), 15); kk = ks[:, :, None, :]
        com = np.take_along_axis(com, kk, 2)[:, :, 0]; late = np.take_along_axis(late, kk, 2)[:, :, 0]
        Ls = np.take_along_axis(L, kk, 2)[:, :, 0]; cell = np.take_along_axis(R, kk, 2)[:, :, 0]
        ev = np.take_along_axis(es, ks[:, :, None, None, :], 3)[:, :, :, 0]
        a, g, e = np.nonzero(late); XC[a, g, :, Ls[a, g, e]] = 0
        X[ci] = XC
        best = np.full((N, 8, W), E, np.int64); np.minimum.at(best, (ai, gi, cell), lane + np.zeros_like(cell))
        win = np.take_along_axis(best, cell, 2) == lane
        XB = X[bi]; a, g, e = np.nonzero(win & com); c = cell[a, g, e]
        XB[a, g, :, c] = (XB[a, g, :, c] + ev[a, g, :, e]) >> 1
        X[bi] = XB
        if t < RO - 1:
            a, g, e = np.nonzero(win & (com | late)); PB[a, g, ks[a, g, e], cell[a, g, e]] = W
            a, g, e = np.nonzero(win); PB[a, g, (e + t) % 16, cell[a, g, e]] = q[a, g, e]
            P[bi] = PB
        v = np.where((rows == kk) & com[:, :, None], L, R) + M * np.where(orphan[:, :, None], 255 - y, y) + 1
        R = np.where(v >= W, v - W, v); z = y
    return {"xo": X.reshape(N, 128, W).astype(np.float32).astype(BF), "ro": R.reshape(N, 128, E).astype(np.float32), "zo": z.reshape(N, 128, E).astype(np.float32).astype(BF)}

@@ -1,0 +1,771 @@
+from concourse.bass import DstId, RemoteDMATransfer
+from concourse.mybir import AluOpType as ALU, ActivationFunctionType as ACT
+
+N, W, E, RO = 4, 1536, 192, 4
+PAD = 16
+YC, ZC = PAD + W, PAD + W + E
+SEG = [8 * b * (b + 1) for b in range(13)]
+MAGIC = 12582912.0
+CFG = {
+    "LG0": [("s", 0, 48), ("v", 96, 144), ("s", 48, 96), ("v", 144, 192)],
+    "LGN": [("s", 0, 64), ("s", 64, 128), ("s", 128, 192)],
+    "XG0": [("s", 0, 48), ("s", 96, 144), ("v", 48, 96), ("s", 144, 192)],
+    "XGN": [("s", 0, 64), ("v", 64, 96), ("s", 96, 160), ("s", 160, 192)],
+    "EG": [(0, 32, "p", 3), (32, 96, "v"), (96, 144, "v"), (144, 192, "v")],
+    "VD": [(0, 96), (96, 192)],
+    "YBS": 144,
+    "PV": (6, 8),
+    "PV4": (0, 6),
+    "PVL": ((6, 9), (3, 3)),
+    "ONS": "ek",
+    "SUMS": [(32, 96), (96, 192)],
+}
+FOUND = {}
+GAP = 100.0
+CFG.update({"SEED": 1, "TURNS": 600, "NOISE": 4000.0, "SLACK": 100.0, "SPAN": 8000.0})
+CYC, GAT, SCA, PEC, HOP, VFIX, SFIX = 1.04, 1.56, 3.8, 0.52, 80.0, 10.0, 100.0
+
+F32, F16, BF, I32, U16 = "float32", "float16", "bfloat16", "int32", "uint16"
+SCRATCH = {}
+for _n, _w, _d in [
+    ("sti", 1728, I32), ("sth", 1728, F16), ("stx", 1728, BF), ("lah", 1728, F16), ("lax", 1728, BF),
+    ("ox", 1536, BF), ("lox", 1536, BF), ("orz", 384, F32), ("lorz", 384, F32), ("zb", 192, BF),
+    ("P", ZC, F32), ("X", ZC + E, BF), ("M8", W, BF),
+    ("GL", 3072, F16), ("GX", 3072, BF), ("MX", 3072, BF), ("MN", 3072, BF),
+    ("YB", 3072, BF), ("YS", 3072, BF), ("DF", 3072, BF), ("AB", 3072, BF), ("SG", 3072, BF),
+    ("U5", 1248, BF), ("U4", 1248, BF), ("F5", 1248, BF), ("F4", 1248, BF), ("MS", 1248, BF),
+    ("R16", E, F16), ("Ru", E, U16), ("L16", E, F16), ("U", E, BF), ("UR", E, F32), ("UI", E, BF), ("FR", E, F16),
+    ("Rp", E, F16), ("Rpu", E, U16), ("Lu", E, U16), ("XQ", E, BF), ("o255", E, BF), ("uu", E, BF),
+    ("sg1", E, BF), ("sg2", E, BF), ("qmB", E, BF), ("aa", E, F32), ("s1", E, BF), ("s2", E, BF), ("key", E, F32),
+    ("kT", E, F32), ("mx", E, F32), ("mb", E, F32), ("oh", E, BF), ("PB", 2 * E, F16),
+    ("PC", 2 * E, F16), ("oc", E, BF), ("t1", E, F32), ("A1", E, F32), ("Lo", E, F32), ("m1", E, F32),
+    ("evd", E, BF), ("old", E, BF), ("nw", E, BF), ("zero", E, BF), ("rn", E, F32), ("w5", E, F16), ("w4", E, F16),
+    ("tf", 352, F32), ("ti", 32, I32), ("tu", 128, U16), ("segu", 4, U16),
+    ("IX", E, BF), ("XI", E, BF), ("XIu", E, U16), ("XS", 128, BF), ("UQ", 128, BF), ("VQ", 528, BF), ("X16", 208, BF),
+    ("col", 64, F32), ("M16", 16, F32), ("IW", 224, BF), ("nIW", 224, BF), ("hIW", 224, BF), ("n16", 128, BF),
+    ("wI", 7 * 128, BF), ("nON", 128, BF), ("ONB", 128, BF), ("TL", 128, BF), ("TLa", 128, BF),
+    ("W0", 144, BF), ("WN", 144, BF), ("WN16", 144, BF), ("WNn", 144, BF), ("WNB", 144, BF),
+    ("SK", 2048, BF), ("c16", 5 * E, F16), ("cb", 5 * E, BF), ("cT", 32, F16),
+    ("Dm", 208, BF), ("Cap", 208, F32), ("r0", 1024, BF), ("rB", 1024, BF),
+]:
+    SCRATCH[_n] = ("sbuf", [128, _w], _d)
+for _n in range(8):
+    SCRATCH["p%d" % _n] = ("psum", [128, 512], F32)
+SEMAPHORES = (["cv", "cs", "ct", "cg"] + ["d%d" % _n for _n in range(28)] + ["l%d" % _n for _n in range(8)]
+              + ["%s%d" % (_k, _n) for _k in ("ah", "ax", "ao", "ar") for _n in range(N)])
+
+
+def A(name, lo, hi, step=1, p0=0, p1=128):
+    return (name, lo, hi, step, p0, p1)
+
+
+def IND(win, off):
+    return ("*", win, off)
+
+
+def width(a):
+    return 16 * (a[2][2] - a[2][1]) if a[0] == "*" else -(-(a[2] - a[1]) // abs(a[3]))
+
+
+def narrow(*aps):
+    return 0.5 if all(SCRATCH[a[0]][2] in (F16, BF, U16) for a in aps) else 1.0
+
+
+def in_psum(a):
+    return SCRATCH[a[0]][0] == "psum"
+
+
+def build(rank, T, topo):
+    ops = []
+    cnt = {"d": 0, "l": 0}
+    sent = {}
+    LG0, LGN, XG0, XGN, EG, VD, YBS, PV, PV4 = [CFG[k] for k in ("LG0", "LGN", "XG0", "XGN", "EG", "VD", "YBS", "PV", "PV4")]
+
+    def ap(a):
+        if not isinstance(a, tuple):
+            return a
+        if a[0] == "*":
+            return ap(a[1]).indirect(ap(a[2]))
+        n, lo, hi, st, p0, p1 = a
+        if st < 0:
+            return T[n][p0:p1, hi - 1:(lo - 1 if lo > 0 else None):st]
+        return T[n][p0:p1, lo:hi:st] if st != 1 else T[n][p0:p1, lo:hi]
+
+    def op(q, fns, out, ins, cost, sem=None, lat=0.0, after=()):
+        rd, wr = [], []
+        for a in ins:
+            if isinstance(a, tuple):
+                rd += [a[1], a[2]] if a[0] == "*" else [a]
+        if isinstance(out, tuple):
+            if out[0] == "*":
+                wr.append(out[1])
+                rd.append(out[2])
+            else:
+                wr.append(out)
+        ops.append({"q": q, "fn": fns, "rd": rd, "wr": wr, "sem": sem, "cost": cost, "lat": lat, "after": list(after)})
+
+    def cost(o, i, per, fix=VFIX):
+        if o[0] == "*":
+            return 60 + width(o) * SCA * CYC
+        if i[0] == "*":
+            return 60 + width(o) * GAT * CYC
+        return max(64, width(o) * per) * CYC + fix
+
+    def rate(o, *i):
+        return 1.0 if "*" in (o[0], i[0][0]) else narrow(o, *i)
+
+    def cp(o, i):
+        op("v", [lambda e: e.tensor_copy(ap(o), ap(i))], o, [i], cost(o, i, rate(o, i)))
+
+    def tt(o, a, b, f):
+        per = 1.0 if "*" in (o[0], a[0]) or in_psum(a) or in_psum(b) else 2.0
+        op("v", [lambda e: e.tensor_tensor(ap(o), ap(a), ap(b), f)], o, [a, b], cost(o, a, per))
+
+    def ts(o, a, s1, f0, s2=None, f1=None):
+        if f1 is None:
+            op("v", [lambda e: e.tensor_scalar(ap(o), ap(a), ap(s1), None, f0)], o, [a, s1], cost(o, a, rate(o, a)))
+        else:
+            op("v", [lambda e: e.tensor_scalar(ap(o), ap(a), ap(s1), ap(s2), f0, f1)], o, [a, s1, s2], cost(o, a, rate(o, a)))
+
+    def scan(o, d0, d1, f0, f1, init=0.0):
+        op("v", [lambda e: e.tensor_tensor_scan(ap(o), ap(d0), ap(d1), init, f0, f1)], o, [d0, d1], cost(o, d0, narrow(o, d0, d1)))
+
+    def vt(o, i):
+        op("v", [lambda e: e.transpose(ap(o), ap(i))], o, [i], cost(o, i, narrow(o, i)))
+
+    def ms(o, c):
+        op("v", [lambda e: e.memset(ap(o), c)], o, [], cost(o, o, narrow(o)))
+
+    def act(o, i, f, bias=0.0, scale=1.0):
+        if f == ACT.Copy:
+            op("s", [lambda e: e.activation(ap(o), ap(i), f, scale=ap(scale))], o, [i, scale], cost(o, i, 1.0, SFIX))
+        else:
+            op("s", [lambda e: e.activation(ap(o), ap(i), f, bias=ap(bias), scale=ap(scale))], o, [i, bias, scale], cost(o, i, 1.0, SFIX))
+
+    def mm(o, terms, start=True, stop=True):
+        fns = [lambda e, l=l, r=r, j=j: e.matmul(ap(o), ap(l), ap(r), start and j == 0, stop and j == len(terms) - 1)
+               for j, (l, r) in enumerate(terms)]
+        op("t", fns, o, [x for lr in terms for x in lr], sum(max(min(64, width(l)), width(r)) for l, r in terms) * PEC, lat=60.0)
+
+    def iota(o, pat, base, mult, whole=False):
+        if whole:
+            op("g", [lambda e: e.iota(ap(o), pat, base, mult)], o, [], 130.0)
+        else:
+            op("g", [lambda e: e.iota(ap(o), pat, base, mult, allow_small_or_imprecise_dtypes=True)], o, [], 130 + 2 * CYC * width(o))
+
+    def dma(q, o, i, lat=2600.0):
+        s = "d%d" % cnt["d"]
+        cnt["d"] += 1
+        op(q, [lambda e: e.dma_start(ap(o), ap(i))], o, [i], 100.0, (s, 16), lat)
+
+    me = T.cores[rank]
+    others = [(rank + j) % N for j in (1, 2, 3)]
+    far = [d for d in others if T.cores[d] not in topo.cores_of(me)]
+    near = [d for d in others if d not in far]
+    NE = 4
+    eng, used = {}, []
+    for j, d in enumerate(far):
+        es = topo.engines(me, T.cores[d])
+        eng[d] = es[j * NE:(j + 1) * NE]
+        used += es
+    spare = [x for x in topo.engines(me, T.cores[near[0]]) if x not in used]
+
+    def send(items):
+        s = "l%d" % cnt["l"]
+        cnt["l"] += 1
+        srcs = [A(src, d * w, (d + 1) * w) for d, src, dst, w, kind, es in items]
+
+        def fn(e):
+            trs = []
+            for (d, src, dst, w, kind, es), a in zip(items, srcs):
+                rid, pid = topo.addr(T.cores[d], me)
+                trs.append(RemoteDMATransfer(dst_ids=[DstId(rid=rid, pnc=pid)], dma_engine_mask=sum(1 << x for x in es),
+                                             remote_sem=T.sem["%s%d" % (kind, rank)], src=ap(a),
+                                             dst=ap(A(dst, rank * w, (rank + 1) * w))))
+            e.remote_dma_fused(trs, local_sem=T.sem[s])
+        for it in items:
+            sent[(it[4], it[0] in far)] = len(ops)
+        op("g", [fn], None, srcs, 1000.0, (s, -NE * len(items)), 4500.0)
+
+    def arrive(kind, s, dst, w):
+        op("a", [], A(dst, s * w, (s + 1) * w), [], 0.0, ("%s%d" % (kind, s), NE), after=[sent[(kind, s in far)]])
+
+    def gather(q, o, win, off):
+        if q == "v":
+            cp(o, IND(win, off))
+        else:
+            act(o, IND(win, off), ACT.Copy)
+
+    ONS = CFG["ONS"]
+
+    def copy(name, o, i, scale=None):
+        if name in ONS:
+            act(o, i, ACT.Copy, scale=1.0 if scale is None else scale)
+        elif scale is None:
+            cp(o, i)
+        else:
+            ts(o, i, scale, ALU.mult)
+
+    def rounded_to(name, o, i):
+        if name in ONS:
+            act(L("rn"), i, ACT.Identity, bias[MAGIC])
+            act(o, L("rn"), ACT.Identity, bias[-MAGIC])
+        else:
+            ts(o, i, MAGIC, ALU.add, -MAGIC, ALU.add)
+
+    I, SH, BK = A("IW", 0, 128), A("IW", 96, 224), A("IW", 32, 160)
+    nI, nSH = A("nIW", 0, 128), A("nIW", 96, 224)
+    hI, hSH, hBK = A("hIW", 0, 128), A("hIW", 96, 224), A("hIW", 32, 160)
+    I6, I768, nI768, nI2048, I8192, nI1024, I2048 = [A("wI", 128 * j, 128 * j + 128) for j in range(7)]
+    nSH16, nON, ONB, TL = A("n16", 0, 128), A("nON", 0, 128), A("ONB", 0, 128), A("TL", 0, 128)
+    pcol, kcol, s16, s16p, sbk, sbkp, nk, asc, k17 = [A("col", j, j + 1) for j in range(9)]
+    bias = {}
+    for j, v in enumerate((-1.0, 3.0, 1.0, 255.0, -1534.5, 0.5, -2048.0, -1535.0, MAGIC, -MAGIC)):
+        bias[v] = A("col", 16 + j, 17 + j)
+
+    def c16(j, lo=0, hi=E):
+        return A("c16", j * E + lo, j * E + hi)
+
+    def cb(j, lo=0, hi=E):
+        return A("cb", j * E + lo, j * E + hi)
+
+    def tf(j, n=12):
+        return A("tf", 16 * j, 16 * j + n)
+
+    def tu(j):
+        return A("tu", 16 * j, 16 * j + 12)
+    iT, dN, i8, qT, qm, orT, tq, bq, b5, b4, ncT, tb, td, te = [tf(j) for j in range(14)]
+    v5, v4, ta, tc = [[tf(j, 16), tf(j + 1, 16)] for j in range(14, 22, 2)]
+    qu, c5u, ju, lku, xlu, l4u = [tu(j) for j in range(6)]
+    Xw, Xc, Xs, Pw, Ps = A("X", PAD, ZC + E), A("X", PAD, YC), A("X", 0, ZC), A("P", PAD, YC), A("P", 0, ZC)
+    yC, yB = A("X", YC, ZC), A("X", ZC, ZC + E)
+
+    def L(n, lo=0, hi=E):
+        return A(n, lo, hi)
+
+    def ps(b, lo, hi, step=1, p0=0, p1=128):
+        return A("p%d" % b, lo, hi, step, p0, p1)
+
+    def tconv(o, w, src, n, first=()):
+        mm(o, list(first) + [(A(w, 16 - a, 144 - a), A(src[0], src[1] + a, src[1] + n, 16)) for a in range(16)])
+
+    order = far + near + [rank]
+    for j, d in enumerate(order):
+        dma("y", A("sti", d * 432, d * 432 + 384), T.lk[32 * d:32 * d + 32, :], 2600.0 + 700 * j)
+        dma("s", A("sti", d * 432 + 384, d * 432 + 432), T.rd[32 * d:32 * d + 32, :])
+    for j, d in enumerate(near + far + [rank]):
+        dma("y", A("stx", d * 432, d * 432 + 384), T.x0[32 * d:32 * d + 32, :], 5000.0 + 400 * j)
+        dma("s", A("stx", d * 432 + 384, d * 432 + 432), T.z0[32 * d:32 * d + 32, :])
+    iota(A("ti", 0, 1), [[0, 1]], 0, 1, True)
+    iota(L("IX"), [[1, E]], 0, -1)
+    iota(A("UQ", 0, 128), [[1, 4], [4, 32]], 0, -1)
+    iota(A("XS", 0, 128), [[16, 8], [0, 16]], 0, 0)
+    iota(A("X16", 0, 208), [[0, 13], [1, 16]], 0, 0)
+    for d in order:
+        cp(A("sth", d * 432, d * 432 + 432), A("sti", d * 432, d * 432 + 432))
+    send([(d, "sth", "lah", 432, "ah", eng[d]) for d in far])
+    send([(near[0], "sth", "lah", 432, "ah", spare[0::2]), (near[0], "stx", "lax", 432, "ax", spare[1::2])])
+    send([(d, "stx", "lax", 432, "ax", eng[d]) for d in far])
+    iota(A("M8", 0, W), [[0, E], [1, 8]], 0, 0)
+    iota(A("VQ", 0, 528), [[1, 528]], -3, -4)
+    for v in bias:
+        ms(bias[v], v)
+    cp(pcol, A("ti", 0, 1))
+    ts(A("ti", 1, 2), A("ti", 0, 1), 15, ALU.bitwise_and)
+    cp(kcol, A("ti", 1, 2))
+    tt(s16, pcol, kcol, ALU.subtract)
+    ts(s16p, s16, 16.0, ALU.add)
+    ts(A("ti", 2, 3), s16, 96.0, ALU.add)
+    ts(A("ti", 3, 4), A("ti", 2, 3), 127, ALU.bitwise_and)
+    cp(sbk, A("ti", 3, 4))
+    ts(sbkp, sbk, 16.0, ALU.add)
+    ts(nk, kcol, -1.0, ALU.mult)
+    ts(asc, kcol, 15.0, ALU.is_equal, 65536.0, ALU.add)
+    ts(k17, kcol, -1.0, ALU.mult, 17.0, ALU.add)
+    ts(A("IW", 0, 128), A("IX", 0, 128), 0.0, ALU.is_equal)
+    ts(A("IW", 128, 224), A("IX", 0, 96), 0.0, ALU.is_equal)
+    ts(L("XI"), L("IX"), pcol, ALU.add)
+    ts(A("M16", 0, 16), A("XI", 0, 16), kcol, ALU.is_equal)
+    ts(A("UQ", 0, 128), A("UQ", 0, 128), 0.0, ALU.is_equal)
+    act(A("nIW", 0, 224), A("IW", 0, 224), ACT.Copy, scale=-1.0)
+    act(A("hIW", 0, 224), A("IW", 0, 224), ACT.Copy, scale=0.5)
+    for a, v in ((nI2048, -2048.0), (I6, 6.0), (I768, 768.0), (nI768, -768.0), (I8192, 8192.0), (nI1024, -1024.0), (I2048, 2048.0)):
+        act(a, I, ACT.Copy, scale=v)
+    act(nSH16, SH, ACT.Copy, scale=-16.0)
+    for k in range(16):
+        ts(A("SK", 128 * k, 128 * k + 128), I, A("M16", k, k + 1), ALU.mult)
+    ts(nON, A("XS", 0, 128), s16, ALU.is_equal, -1.0, ALU.mult)
+    ts(ONB, A("XS", 0, 128), sbk, ALU.is_equal)
+    ts(A("TLa", 0, 128), A("IX", 0, 128), 0.0, ALU.is_gt, 2048.0, ALU.mult)
+    tt(A("TLa", 0, 128), A("TLa", 0, 128), nON, ALU.mult)
+    tt(TL, A("TLa", 0, 128), nI2048, ALU.subtract)
+    ts(c16(0), L("XI"), 1728.0, ALU.add)
+    ms(A("r0", 0, 1024), 1.0)
+    ms(A("r0", 0, 1024, 16), 0.0)
+    act(A("rB", 0, 1024), A("r0", 0, 1024), ACT.Identity, 256.0, -256.0)
+    ms(A("P", 0, PAD), 0.0)
+    ms(A("P", YC, ZC), 0.0)
+    ms(A("X", 0, PAD), 0.0)
+    ms(yC, 0.0)
+    ts(A("WN", 0, 144), A("XI", 0, 144), s16p, ALU.is_equal)
+    ts(A("WNB", 0, 144), A("XI", 0, 144), sbkp, ALU.is_equal)
+    act(A("WN16", 0, 144), A("WN", 0, 144), ACT.Copy, scale=16.0)
+    act(A("WNn", 0, 144), A("WN", 0, 144), ACT.Copy, scale=-1.0)
+    for c in EG:
+        ms(cb(4, c[0], c[1]), -16.0 if c[2] == "v" else 0.0)
+    for lo in range(0, 16 * YBS, 256):
+        act(A("YS", lo, lo + 256), A("r0", 0, 256), ACT.Copy, scale=0.0)
+    ms(A("MS", 0, 1248), 0.0)
+    act(A("MS", 0, 15), A("M16", 1, 16), ACT.Copy, scale=-2048.0)
+    for b in range(1, 12):
+        act(A("MS", SEG[b] + 16 * b - 1, SEG[b + 1] - 1), A("M16", 0, 16), ACT.Copy, scale=-2048.0)
+    for b in range(12):
+        ms(A("MS", SEG[b + 1] - 1, SEG[b + 1]), 4096.0)
+    ts(c16(1), L("XI"), 512.0, ALU.add)
+    ts(c16(2), L("XI"), 1552.0, ALU.add)
+    ts(c16(3), L("XI"), 8.0, ALU.mult, 2048.0, ALU.add)
+    ms(c16(4), -767.0)
+    for j, v in enumerate((-0.25, 16.0, 65536.0)):
+        ms(cb(j), v)
+    ts(cb(3), L("XI"), 0.0, ALU.mult, k17, ALU.add)
+    ms(L("zero"), 0.0)
+    cp(L("XIu"), L("XI"))
+    ts(A("Dm", 0, 208), A("X16", 0, 208), kcol, ALU.is_equal)
+    ts(A("Cap", 0, 208), A("Dm", 0, 208), -2048.0, ALU.mult, 2048.0, ALU.add)
+    ts(iT, A("XI", 0, 12), 16.0, ALU.mult, kcol, ALU.add)
+    ts(dN, iT, -1.0, ALU.mult, 4096.0 - YC, ALU.add)
+    ts(i8, iT, 8.0, ALU.mult)
+    ts(qT, iT, 8.0, ALU.mult)
+    ms(qm, 0.0)
+    cp(qu, qT)
+    ms(A("tf", 224, 288), 0.0)
+    ts(A("VQ", 0, 528), A("VQ", 0, 528), 0.0, ALU.is_equal)
+    for p in range(2):
+        ts(A("cT", 12 * p, 12 * p + 6), A("tf", 6 * p, 6 * p + 6), float(YC), ALU.add)
+        ts(A("cT", 12 * p + 6, 12 * p + 12), A("tf", 6 * p, 6 * p + 6), 16.0, ALU.mult)
+        ts(A("col", 32 + p, 33 + p), kcol, 5.0, ALU.min, 1.0 + 6 * p, ALU.add)
+        ts(A("col", 34 + p, 35 + p), A("col", 32 + p, 33 + p), 1.0, ALU.add, A("col", 32 + p, 33 + p), ALU.mult)
+        ts(A("segu", 2 * p, 2 * p + 1), A("col", 34 + p, 35 + p), 8.0, ALU.mult, -1.0 - SEG[6 * p], ALU.add)
+    ts(A("col", 36, 37), sbk, 64.0, ALU.add)
+    ts(A("ti", 4, 5), A("col", 36, 37), 0.0, ALU.add)
+    ts(A("ti", 5, 6), A("ti", 4, 5), 127, ALU.bitwise_and)
+    ts(A("col", 37, 38), A("ti", 5, 6), 16.0, ALU.add)
+    ts(A("col", 38, 39), A("M16", 0, 1), 0.5, ALU.mult)
+    ts(A("W0", 0, 144), A("XI", 0, 144), A("col", 37, 38), ALU.is_equal, A("col", 38, 39), ALU.mult)
+
+    def unpack(kind, own, land, bank):
+        for s in [rank] + near + far:
+            if s != rank:
+                arrive(kind, s, land, 432)
+            src = own if s == rank else land
+            h = (s + 2) % N
+            for u in range(4):
+                w = A("UQ", 32 * u, 32 * u + 32)
+                mm(ps(bank + u, 384, 432, 1, 32 * h, 32 * h + 32), [(w, A(src, s * 432 + 384, s * 432 + 432))])
+                mm(ps(bank + u, 0, 384, 1, 32 * s, 32 * s + 32), [(w, A(src, s * 432, s * 432 + 384))])
+    unpack("ah", "sth", "lah", 0)
+    for u in range(4):
+        cp(A("Ru", 48 * u, 48 * u + 48), ps(u, 384, 432))
+        cp(A("R16", 48 * u, 48 * u + 48), ps(u, 384, 432))
+        if u % 2 == 0:
+            act(A("P", PAD + 384 * u, PAD + 384 * u + 384), ps(u, 0, 384), ACT.Copy)
+        else:
+            cp(A("P", PAD + 384 * u, PAD + 384 * u + 384), ps(u, 0, 384))
+    unpack("ax", "stx", "lax", 4)
+    for u in range(4):
+        if u % 2 == 0:
+            act(A("X", PAD + 384 * u, PAD + 384 * u + 384), ps(4 + u, 0, 384), ACT.Copy)
+        else:
+            cp(A("X", PAD + 384 * u, PAD + 384 * u + 384), ps(4 + u, 0, 384))
+        cp(A("X", ZC + 48 * u, ZC + 48 * u + 48), ps(4 + u, 384, 432))
+
+    def locks(chunks):
+        for j, (q, lo, hi) in enumerate(chunks):
+            n, b, o = hi - lo, j % 3, 192 * (j // 3)
+            gather(q, A("GL", 16 * lo, 16 * hi), Pw, L("Ru", lo, hi))
+            mm(ps(b, o, o + n), [(A("SK", 128 * k, 128 * k + 128), A("GL", 16 * lo + k, 16 * hi, 16)) for k in range(16)])
+            if "U" in ONS:
+                act(L("U", lo, hi), ps(b, o, o + n), ACT.Relu, bias[-1535.0])
+            else:
+                ts(L("U", lo, hi), ps(b, o, o + n), float(W), ALU.is_equal)
+            copy("L", L("L16", lo, hi), ps(b, o, o + n))
+            mm(ps(b, o + 64, o + 64 + n), [(I, c16(0, lo, hi)), (nI, L("R16", lo, hi)), (TL, L("U", lo, hi))])
+            tt(L("UR", lo, hi), L("U", lo, hi), L("R16", lo, hi), ALU.mult)
+            if "F" in ONS:
+                act(L("FR", lo, hi), ps(b, o + 64, o + 64 + n), ACT.Relu, bias[-2048.0])
+            else:
+                ts(L("FR", lo, hi), ps(b, o + 64, o + 64 + n), -2048.0, ALU.add, 0.0, ALU.max)
+            mm(ps(b, o + 128, o + 128 + n), [(I, c16(0, lo, hi)), (nI2048, L("U", lo, hi)), (nON, L("FR", lo, hi))])
+            tt(L("Rp", lo, hi), ps(b, o + 128, o + 128 + n), L("UR", lo, hi), ALU.max)
+            cp(L("Rpu", lo, hi), L("Rp", lo, hi))
+
+    def features(chunks):
+        gather("s" if "q" in ONS else "v", L("XQ"), Xc, qu)
+        tconv(ps(5, 16, 28), "WN", L("XQ"), E)
+        empty = len(ops) - 1
+        mm(ps(7, 192, 384), [(ONB, L("XQ"))])
+        act(orT, ps(5, 16, 28), ACT.Relu, bias[1.0], -1.0)
+        act(L("o255"), ps(7, 192, 384), ACT.Relu, bias[255.0], -255.0)
+        tt(tq, orT, qm, ALU.mult)
+        tt(bq, qT, tq, ALU.subtract)
+        for (q, lo, hi) in chunks:
+            n = 16 * (hi - lo)
+            g, a, b = A("GX", 16 * lo, 16 * hi), A("MX", 16 * lo, 16 * hi), A("MN", 16 * lo, 16 * hi)
+            gather(q, g, Xw, L("Rpu", lo, hi))
+            scan(a, A("r0", 0, n), g, ALU.mult, ALU.max)
+            scan(b, A("rB", 0, n), g, ALU.add, ALU.min)
+        for (q, lo, hi) in chunks:
+            a, b = A("MX", 16 * lo + 15, 16 * hi, 16), A("MN", 16 * lo + 15, 16 * hi, 16)
+            mm(ps(3, lo, hi), [(I, cb(0, lo, hi)), (hSH, a), (hSH, b)])
+            mm(ps(4, lo, hi), [(I, cb(0, lo, hi)), (hI, a), (hI, b)])
+        for x in ("MX", "MN"):
+            mm(ps(5, 0, 12), ([(I, cb(0, 0, 12))] if x == "MX" else [])
+               + [(A("W0", 16 - a, 144 - a), A(x, 16 * a + 15, 3072, 256)) for a in range(16)], x == "MX", x == "MN")
+            ops[-1]["after"].append(empty if x == "MX" else len(ops) - 4)
+        mm(ps(6, 192, 384), [(nI, L("XI")), (nI2048, L("U"))])
+        act(L("UI"), ps(6, 192, 384), ACT.Relu, bias[-2048.0], -1.0)
+        mm(ps(2, 320, 512), [(SH, L("L16")), (SH, L("UI"))])
+        mm(ps(6, 0, 192), [(SH, L("R16")), (I, cb(1))])
+        cp(L("Lu"), ps(2, 320, 512))
+
+    def primary(t):
+        ts(yC, ps(3, 0, E), MAGIC, ALU.add, -MAGIC, ALU.add)
+        act(A("YS", 0, 16 * YBS, 16), A("X", YC, YC + YBS), ACT.Copy)
+        rows = [c[:2] for c in EG if c[2] != "p"]
+        for lo, hi in rows:
+            if lo >= YBS:
+                gather("s", A("YB", 16 * lo, 16 * hi), yC, L("XIu", lo, hi))
+        rounded_to("y", yB, ps(4, 0, E))
+        for lo, hi in rows:
+            if lo < YBS:
+                scan(A("YB", 16 * lo, 16 * hi), A("r0", 0, 16 * (hi - lo)), A("YS", 16 * lo, 16 * hi), ALU.mult, ALU.add)
+        tt(A("ti", 0, 12), ps(5, 0, 12), orT, ALU.mult)
+        ts(A("ti", 16, 28), A("ti", 0, 12), 7, ALU.bitwise_and)
+        tt(qT, A("ti", 16, 28), bq, ALU.add)
+        cp(qu, qT)
+        cp(IND(Xc, qu), yC)
+        tt(qm, qT, i8, ALU.subtract)
+        mm(ps(3, 192, 384), [(I, L("o255")), (nI, yB)])
+        act(L("uu"), ps(3, 192, 384), ACT.Abs)
+        mm(ps(4, 192, 384), [(I, L("R16")), (I6, L("uu"))])
+        mm(ps(3, 192, 384), [(I, L("L16")), (I6, L("uu"))])
+        act(L("sg1"), ps(4, 192, 384), ACT.Sign, bias[-1534.5])
+        act(L("sg2"), ps(3, 192, 384), ACT.Sign, bias[-1534.5])
+        mm(ps(6, 192, 384), [(I, L("R16")), (I6, L("uu")), (I, c16(4)), (nI768, L("sg1"))])
+        mm(ps(7, 0, 192), [(I, L("L16")), (nI, L("R16")), (I768, L("sg1")), (nI768, L("sg2"))])
+        if t < RO - 1:
+            gather("s", L("qmB"), A("M8", 0, W), qu)
+            mm(ps(7, 192, 384), [(I, c16(3)), (nI2048, A("Dm", t, t + E)), (BK, L("qmB"))])
+
+    def compare(lo, hi, who, how="s"):
+        b = [j for j, v in enumerate(VD) if v[0] <= lo < v[1]][0]
+        off, n = lo - VD[b][0], hi - lo
+        d, a, s = A("DF", 16 * lo, 16 * hi), A("AB", 16 * lo, 16 * hi), A("SG", 16 * lo, 16 * hi)
+        if who == "p":
+            gather("s", d, A("X", PAD, ZC), L("Lu", lo, hi))
+            for k in range(16):
+                mm(ps(how, n * k, n * k + n), [(nI, A("X", YC + lo, YC + hi)), (I, A("DF", 16 * lo + k, 16 * hi, 16))])
+            act(s, ps(how, 0, 16 * n), ACT.Sign, bias[0.5])
+            act(a, ps(how, 0, 16 * n), ACT.Abs)
+            mm(ps(b, off, off + n), [(nSH16, L("U", lo, hi))]
+               + [(A("WN", 16 - k, 144 - k), A("SG", 16 * lo + n * k, 16 * lo + n * k + n)) for k in range(16)])
+            mm(ps(b, 96 + off, 96 + off + n), [(I, cb(2, lo, hi)), (I, cb(3, lo, hi))]
+               + [(A("WN16", 16 - k, 144 - k), A("AB", 16 * lo + n * k, 16 * lo + n * k + n)) for k in range(16)])
+            return
+        tt(d, IND(A("X", PAD, ZC), L("Lu", lo, hi)), A("YB", 16 * lo, 16 * hi), ALU.subtract)
+        if who == "v":
+            ts(s, d, 0.0, ALU.is_ge, 2.0, ALU.mult)
+        else:
+            act(s, d, ACT.Sign, bias[0.5])
+        act(a, d, ACT.Abs)
+        for l0, h0 in CFG["SUMS"]:
+            if h0 == hi:
+                off, n = l0 - VD[b][0], hi - l0
+                mm(ps(b, off, off + n), [(I, cb(4, l0, hi)), (nSH16, L("U", l0, hi))]
+                   + [(A("WN", 16 - k, 144 - k), A("SG", 16 * l0 + k, 16 * hi, 16)) for k in range(16)])
+                mm(ps(b, 96 + off, 96 + off + n), [(I, cb(2, l0, hi)), (I, cb(3, l0, hi))]
+                   + [(A("WN16", 16 - k, 144 - k), A("AB", 16 * l0 + k, 16 * hi, 16)) for k in range(16)])
+
+    def verdict(b):
+        lo, hi = VD[b]
+        n = hi - lo
+        sg = ps(b, 0, n)
+        act(L("aa", lo, hi), sg, ACT.Abs, asc, asc)
+        act(L("s2", lo, hi), sg, ACT.Sign, bias[3.0])
+        act(L("s1", lo, hi), sg, ACT.Sign, bias[-1.0])
+        tt(L("key", lo, hi), ps(b, 96, 96 + n), L("aa", lo, hi), ALU.min)
+        mm(ps(b, 192, 192 + n), [(nSH, L("L16", lo, hi)), (nSH, L("UI", lo, hi)), (I, c16(1, lo, hi)), (nI1024, L("s2", lo, hi))])
+        mm(ps(b, 288, 288 + n), [(I2048, L("s2", lo, hi)), (I2048, L("s1", lo, hi))])
+        act(ps(b, 384, 384 + n), ps(b, 192, 192 + n), ACT.Relu)
+        vt(L("kT", lo, hi), L("key", lo, hi))
+        scan(L("mx", lo, hi), A("r0", 0, n), L("kT", lo, hi), ALU.mult, ALU.max)
+        scan(A("mb", lo, hi, -1), A("r0", 0, n), A("mx", lo, hi, -1), ALU.mult, ALU.max)
+        vt(ps(2, lo, hi), L("mb", lo, hi))
+        tt(L("oh", lo, hi), L("key", lo, hi), ps(2, lo, hi), ALU.is_equal)
+        tt(A("PB", 2 * lo, 2 * lo + n), ps(6, lo, hi), L("oh", lo, hi), ALU.mult)
+        tt(A("PB", 2 * lo + n, 2 * hi), ps(b, 288, 288 + n), L("oh", lo, hi), ALU.mult)
+        tt(A("PC", 2 * lo, 2 * lo + n), ps(b, 384, 384 + n), L("oh", lo, hi), ALU.mult)
+        copy("k", A("PC", 2 * lo + n, 2 * hi), L("oh", lo, hi), nk)
+
+    def half(a, p):
+        return A(a[0], a[1] + 6 * p, a[1] + 6 * p + 6)
+
+    def first(p, since, o, u, bank, copy, val, col, sb, t0, t1, nv):
+        b0 = (96 * p - since) // 16
+        at = SEG[6] * p - SEG[b0]
+        top = min(since + 16 * nv, 96 * p + 96)
+        if top > 96 * p:
+            act(L(copy, 96 * p, top), ps(bank, 96 * p, top), ACT.Copy)
+        if nv < b0 + 6:
+            act(half(col, p), val, ACT.Copy, scale=-2048.0)
+        if "b" in ONS:
+            act(A(sb[0], sb[1], sb[1] + 6), val, ACT.Copy)
+        else:
+            cp(A(sb[0], sb[1], sb[1] + 6), val)
+        for b in range(b0 + 5, b0 - 1, -1):
+            j, out = b - b0, A(u, at + SEG[b], at + SEG[b + 1])
+            if b >= nv:
+                act(out, ps(bank, since, since + 16 * b + 16), ACT.Abs, A(col[0], col[1] + 6 * p + j, col[1] + 6 * p + j + 1), 2048.0)
+            else:
+                ts(out, A(copy, since, since + 16 * b + 16), A(sb[0], sb[1] + j, sb[1] + j + 1), ALU.not_equal, 2048.0, ALU.mult)
+        lo, hi = at + SEG[b0], at + SEG[b0 + 6]
+        scan(A(o, lo, hi), A(u, lo, hi), A("MS", SEG[b0], SEG[b0 + 6]), ALU.min, ALU.add, 4096.0)
+        tt(t0, IND(A(o, lo, hi), A("segu", b0 // 3, b0 // 3 + 1)), sb, ALU.subtract)
+        tt(half(t1, p), A(t0[0], t0[1], t0[1] + 6), half(dN, p), ALU.max)
+
+    def back(t):
+        last = t == RO - 1
+        n5, n4 = CFG["PVL"] if last else (PV, PV4)
+        for p in range(2):
+            lo, hi = VD[p]
+            c, f = A("PB", 2 * lo, 2 * lo + 96), A("PB", 2 * lo + 96, 2 * hi)
+            o5 = 32 + 16 * p
+            mm(ps(2, lo, hi), [(BK, f)])
+            tconv(ps(5, o5, o5 + 12), "WNB", A("PB", 2 * lo, 2 * hi), 192)
+            mm(ps(3, lo, hi), [(ONB, c)])
+            cp(half(c5u, p), ps(5, o5, o5 + 6))
+            tt(half(ncT, p), ps(5, o5 + 6, o5 + 12), half(dN, p), ALU.max)
+            act(L("oc", lo, hi), ps(2, lo, hi), ACT.Relu, 0.0, 1.0 / 4096)
+            tt(L("t1", lo, hi), ps(7, lo, hi), L("oc", lo, hi), ALU.mult)
+            tt(L("R16", lo, hi), ps(6, 192 + lo, 192 + hi), L("t1", lo, hi), ALU.add)
+            first(p, 0, "F5", "U5", 3, "w5", ps(5, o5, o5 + 6), b5, v5[p], ta[p], tb, n5[p])
+            if not last:
+                cp(L("Ru", lo, hi), L("R16", lo, hi))
+                mm(ps(2, 192 + lo, 192 + hi), [(I8192, A("Dm", t + lo, t + hi)), (BK, f)])
+                act(L("A1", lo, hi), ps(2, 192 + lo, 192 + hi), ACT.Abs, 0.0, 0.375)
+                tt(L("m1", lo, hi), IND(Ps, half(c5u, p)), A("Cap", t + lo, t + hi), ALU.min)
+                tt(L("Lo", lo, hi), ps(7, 192 + lo, 192 + hi), L("A1", lo, hi), ALU.min)
+                ts(half(lku, p), half(tb, p), -1.0, ALU.mult, 4096.0, ALU.add)
+                tt(IND(Ps, half(lku, p)), L("m1", lo, hi), L("Lo", lo, hi), ALU.max)
+        for p in range(2):
+            lo, hi = VD[p]
+            o4 = 384 + 16 * p
+            tconv(ps(6, o4, o4 + 12), "WNn", A("PC", 2 * lo, 2 * hi), 192, [(I, A("cT", 12 * p, 12 * p + 12))])
+            mm(ps(4, lo, hi), [(I, c16(2, lo, hi)), (nON, A("PC", 2 * lo, 2 * lo + 96))])
+            cp(half(ju, p), ps(6, o4 + 6, o4 + 12))
+            first(p, lo, "F4", "U4", 4, "w4", ps(6, o4, o4 + 6), b4, v4[p], tc[p], td, n4[p])
+            ts(half(l4u, p), half(td, p), -1.0, ALU.mult, 4096.0, ALU.add)
+            cp(IND(Xs, half(l4u, p)), L("zero", 0, 96))
+        gather("s" if "e" in ONS else "v", L("evd"), A("DF", 0, 3072), ju)
+        tt(te, tb, ncT, ALU.min)
+        ts(xlu, te, -1.0, ALU.mult, 4096.0, ALU.add)
+        gather("s" if "o" in ONS else "v", L("old"), Xs, c5u)
+        cuts = sorted(set([0, E] + [x for c in EG if c[2] == "p" for x in c[:2]]))
+        for lo, hi in zip(cuts, cuts[1:]):
+            whole = any(c[2] == "p" and c[0] == lo for c in EG)
+            mm(ps(3, 192 + lo, 192 + hi), [(I, cb(0, lo, hi))] + ([] if whole else [(hI, A("X", ZC + lo, ZC + hi))])
+               + [(hBK, L("evd", lo, hi)), (hI, L("old", lo, hi))])
+        ts(L("nw"), ps(3, 192, 384), MAGIC, ALU.add, -MAGIC, ALU.add)
+        cp(IND(Xs, xlu), L("nw"))
+
+    for t in range(RO):
+        locks(LGN if t else LG0)
+        features(XGN if t else XG0)
+        primary(t)
+        for c in EG:
+            compare(*c)
+        for b in range(len(VD)):
+            verdict(b)
+        back(t)
+
+    for d in order:
+        b = (d + 2) % N
+        for j, src in enumerate((L("R16"), yB)):
+            mm(ps(d % 2, 96 * (d // 2) + 48 * j, 96 * (d // 2) + 48 * j + 48),
+               [(A("VQ", 128 * b - u + 3, 128 * b - u + 131), A(src[0], src[1] + 48 * u, src[1] + 48 * u + 48)) for u in range(4)])
+    for d in range(N):
+        act(A("orz", 96 * d, 96 * d + 96), ps(d % 2, 96 * (d // 2), 96 * (d // 2) + 96), ACT.Copy)
+    send([(d, "orz", "lorz", 96, "ar", eng[d]) for d in far] + [(near[0], "orz", "lorz", 96, "ar", spare[0::2])])
+    for j, d in enumerate(order):
+        b = (0, 1, 4, 5)[j]
+        mm(ps(b, 0, 384), [(A("VQ", 128 * d - u + 3, 128 * d - u + 131), A("X", PAD + 384 * u, PAD + 384 * u + 384)) for u in range(4)])
+        o = A("ox", 384 * d, 384 * d + 384)
+        if j % 2 == 0:
+            cp(o, ps(b, 0, 384))
+        else:
+            act(o, ps(b, 0, 384), ACT.Copy)
+        if j == len(far) - 1:
+            send([(x, "ox", "lox", 384, "ao", eng[x]) for x in far])
+        if j == len(far):
+            send([(near[0], "ox", "lox", 384, "ao", spare[0::2])])
+    for s in [rank] + near + far:
+        src = "orz" if s == rank else "lorz"
+        if s != rank:
+            arrive("ar", s, "lorz", 96)
+        dma("y", T.ro[32 * s:32 * s + 32, :], A(src, 96 * s, 96 * s + 48))
+        act(A("zb", 48 * s, 48 * s + 48), A(src, 96 * s + 48, 96 * s + 96), ACT.Copy)
+        dma("y", T.zo[32 * s:32 * s + 32, :], A("zb", 48 * s, 48 * s + 48))
+    for j, s in enumerate([rank] + near + far):
+        if s != rank:
+            arrive("ao", s, "lox", 384)
+        dma("s" if j % 2 == 0 else "y", T.xo[32 * s:32 * s + 32, :], A("ox" if s == rank else "lox", 384 * s, 384 * s + 384))
+    return ops
+
+
+def hazards(ops):
+    hist, out = {}, []
+    for n, o in enumerate(ops):
+        deps = set()
+        touch = [(a, False) for a in o["rd"]] + [(a, True) for a in o["wr"]]
+        for a, w in touch:
+            for (lo, hi, p0, p1, m, mw) in hist.get(a[0], []):
+                if lo < a[2] and a[1] < hi and p0 < a[5] and a[4] < p1 and (w or mw):
+                    deps.add(m)
+        for a in o["wr"]:
+            if abs(a[3]) == 1 and a[5] - a[4] == 128:
+                hist[a[0]] = [h for h in hist.get(a[0], []) if not (a[1] <= h[0] and h[1] <= a[2])]
+        for a, w in touch:
+            hist.setdefault(a[0], []).append((a[1], a[2], a[4], a[5], n, w))
+        deps.discard(n)
+        out.append(deps)
+    return out
+
+
+def place(ops, pred, order, banks):
+    start, end, taken, used = {}, {}, {}, {}
+    for n in order:
+        o = ops[n]
+        t = max([end[m] + d for m, d in pred[n]] + [0.0])
+        c = o["cost"]
+        blocks = [(a, b) for a, b in taken.get(o["q"], []) if b > t]
+        for x in banks[n]:
+            blocks += [(a - GAP, b + GAP) for a, b, e in used.get(x, []) if e != o["q"] and b + GAP > t]
+        blocks.sort()
+        for a, b in blocks:
+            if t + c <= a:
+                break
+            t = max(t, b)
+        start[n], end[n] = t, t + c
+        taken.setdefault(o["q"], []).append((t, t + c))
+        for x in banks[n]:
+            used.setdefault(x, []).append((t, t + c, o["q"]))
+    return start, end
+
+
+def ranked(pred, succ, key):
+    left = [len(p) for p in pred]
+    free = sorted((key[n], n) for n in range(len(pred)) if not left[n])
+    out = []
+    while free:
+        n = free.pop(0)[1]
+        out.append(n)
+        for m, d in succ[n]:
+            left[m] -= 1
+            if not left[m]:
+                free.append((key[m], m))
+        free.sort()
+    return out
+
+
+def arrange(ops):
+    dep = hazards(ops)
+    pred = [[] for o in ops]
+    succ = [[] for o in ops]
+    prev = {}
+    for n, o in enumerate(ops):
+        e = {m: (0.0 if ops[m]["q"] == "t" == o["q"] else ops[m]["lat"] + HOP) for m in dep[n].union(o["after"])}
+        if o["q"] in "gy":
+            if o["q"] in prev:
+                e.setdefault(prev[o["q"]], 0.0)
+            prev[o["q"]] = n
+        for m, d in e.items():
+            pred[n].append((m, d))
+            succ[m].append((n, d))
+    banks = [set(a[0] for a in o["rd"] + o["wr"] if in_psum(a)) for o in ops]
+    key = [0.0] * len(ops)
+    for n in range(len(ops) - 1, -1, -1):
+        key[n] = min([key[m] - d for m, d in succ[n]] + [-ops[n]["lat"]]) - ops[n]["cost"]
+    best, seed = None, CFG["SEED"]
+    key = FOUND.get("key", key)
+    for turn in range(1 if FOUND else CFG["TURNS"]):
+        start, end = place(ops, pred, ranked(pred, succ, key), banks)
+        span = max(end[n] + ops[n]["lat"] for n in end)
+        if best is None or span < best[0]:
+            best = (span, start, end)
+        if span > best[0] + CFG["SLACK"]:
+            end = best[2]
+        back = [-end[n] for n in range(len(ops))]
+        seed = (seed * 1103515245 + 12345) % 2147483648
+        at = best[0] * seed / 2147483648.0
+        for n in range(len(ops)):
+            if abs(end[n] - at) < CFG["SPAN"]:
+                seed = (seed * 1103515245 + 12345) % 2147483648
+                back[n] += CFG["NOISE"] * (seed / 2147483648.0 - 0.5)
+        s2, e2 = place(ops, succ, ranked(succ, pred, back), banks)
+        key = [-e2[n] for n in range(len(ops))]
+    FOUND.setdefault("key", [best[1][n] for n in range(len(ops))])
+    FOUND["span"] = best[0]
+    return [ops[n] for n in sorted(range(len(ops)), key=lambda n: (best[1][n], n))]
+
+
+def waits_of(ops):
+    dep = hazards(ops)
+    bank, known, clock, need = {}, {}, [], []
+    for n, o in enumerate(ops):
+        q = o["q"]
+        deps = set(m for m in dep[n] if q != "t" or ops[m]["q"] != "t")
+        for a in o["rd"] + o["wr"]:
+            if in_psum(a):
+                deps.update(m for e, m in bank.get(a[0], {}).items() if e != q)
+                bank.setdefault(a[0], {})[q] = n
+        kn = known.setdefault(q, {})
+        ws = []
+        for m in sorted(deps, reverse=True):
+            key = ops[m]["q"] if ops[m]["sem"] is None else ops[m]["sem"][0]
+            if kn.get(key, -1) < m:
+                ws.append(m)
+                for k, v in clock[m].items():
+                    kn[k] = max(kn.get(k, -1), v)
+                kn[key] = m
+        clock.append(dict(kn) if q != "a" else {})
+        need.append(ws if q != "a" else [])
+    return need
+
+
+def rank_program(g, core, T, topo):
+    rank = T.rank_of(core)
+    if rank is None:
+        return
+    ops = arrange(build(rank, T, topo))
+    need = waits_of(ops)
+    queue = {"v": g.vector, "s": g.scalar, "t": g.tensor, "g": g, "y": g.sync}
+    waited = set(m for ws in need for m in ws)
+    count, at = {}, {}
+    for n, o in enumerate(ops):
+        q, sem = o["q"], o["sem"]
+        for m in need[n]:
+            queue[q].wait_ge(T.sem[at[m][0]], at[m][1])
+        ins = None
+        for fn in o["fn"]:
+            ins = fn(queue[q])
+        if sem is not None:
+            at[n] = (sem[0], abs(sem[1]))
+            if q != "a" and sem[1] > 0:
+                ins.then_inc(T.sem[sem[0]], 16)
+        elif n in waited:
+            count[q] = count.get(q, 0) + 1
+            at[n] = ("c" + q, count[q])
+            ins.then_inc(T.sem["c" + q], 1)
+    for n, o in enumerate(ops):
+        if o["sem"] is not None and n not in waited:
+            g.sync.wait_ge(T.sem[at[n][0]], at[n][1])

@@ -21,9 +21,9 @@ CFG = {
     "SUMS": [(32, 96), (96, 192)],
 }
 FOUND = {}
-GAP = 100.0
-CFG.update({"SEED": 1, "TURNS": 600, "NOISE": 4000.0, "SLACK": 100.0, "SPAN": 8000.0})
-CYC, GAT, SCA, PEC, HOP, VFIX, SFIX = 1.04, 1.56, 3.8, 0.52, 80.0, 10.0, 100.0
+GAP = 170.0
+CFG.update({"SEED": 1, "TURNS": 700, "NOISE": 4000.0, "SLACK": 100.0, "SPAN": 8000.0})
+CYC, GAT, SCA, PEC, HOP, VFIX, SFIX = 0.95, 1.56, 3.8, 0.5, 150.0, 20.0, 110.0
 
 F32, F16, BF, I32, U16 = "float32", "float16", "bfloat16", "int32", "uint16"
 SCRATCH = {}

@@ -4,36 +4,36 @@ from concourse.mybir import AluOpType as ALU, ActivationFunctionType as ACT
 N, W, E, RO = 4, 1536, 192, 4
 PAD = 16
 YC, ZC = PAD + W, PAD + W + E
-SEG = [8 * b * (b + 1) for b in range(13)]
+SEG = [8 * b * (b + 1) + 2 * b + 4 * (b // 6) for b in range(12)]
 MAGIC = 12582912.0
 CFG = {
     "LG0": [("s", 0, 48), ("v", 96, 144), ("s", 48, 96), ("v", 144, 192)],
     "LGN": [("s", 0, 64), ("s", 64, 128), ("s", 128, 192)],
     "XG0": [("s", 0, 48), ("s", 96, 144), ("v", 48, 96), ("s", 144, 192)],
     "XGN": [("s", 0, 64), ("v", 64, 96), ("s", 96, 160), ("s", 160, 192)],
-    "EG": [(0, 32, "p", 3), (32, 96, "v"), (96, 144, "v"), (144, 192, "v")],
+    "EG": [(0, 32, "p", 2), (32, 96, "v"), (96, 144, "v"), (144, 192, "v")],
     "VD": [(0, 96), (96, 192)],
     "YBS": 144,
-    "PV": (6, 8),
-    "PV4": (0, 6),
-    "PVL": ((6, 9), (3, 3)),
+    "PV": (0, 12),
+    "PV4": (0, 0),
+    "PVL": ((0, 0), (6, 6)),
     "ONS": "ek",
-    "SUMS": [(32, 96), (96, 192)],
+    "SUMS": [(32, 96), (96, 144), (144, 192)],
 }
 FOUND = {}
-GAP = 170.0
-CFG.update({"SEED": 1, "TURNS": 700, "NOISE": 4000.0, "SLACK": 100.0, "SPAN": 8000.0})
-CYC, GAT, SCA, PEC, HOP, VFIX, SFIX = 0.95, 1.56, 3.8, 0.5, 150.0, 20.0, 110.0
+GAP = 240.0
+CFG.update({"SEED": 1, "TURNS": 2000, "NOISE": 3000.0, "SLACK": 60.0, "SPAN": 4000.0})
+CYC, GAT, SCA, PEC, HOP, VFIX, SFIX = 0.92, 1.56, 3.8, 0.46, 220.0, 15.0, 70.0
 
 F32, F16, BF, I32, U16 = "float32", "float16", "bfloat16", "int32", "uint16"
 SCRATCH = {}
 for _n, _w, _d in [
     ("sti", 1728, I32), ("sth", 1728, F16), ("stx", 1728, BF), ("lah", 1728, F16), ("lax", 1728, BF),
     ("ox", 1536, BF), ("lox", 1536, BF), ("orz", 384, F32), ("lorz", 384, F32), ("zb", 192, BF),
-    ("P", ZC, F32), ("X", ZC + E, BF), ("M8", W, BF),
+    ("P", 6160, F32), ("X", 14336, BF), ("M8", W, BF),
     ("GL", 3072, F16), ("GX", 3072, BF), ("MX", 3072, BF), ("MN", 3072, BF),
     ("YB", 3072, BF), ("YS", 3072, BF), ("DF", 3072, BF), ("AB", 3072, BF), ("SG", 3072, BF),
-    ("U5", 1248, BF), ("U4", 1248, BF), ("F5", 1248, BF), ("F4", 1248, BF), ("MS", 1248, BF),
+    ("U5", 1280, BF), ("U4", 1280, BF), ("F5", 1280, BF), ("F4", 1280, BF), ("MS", 1280, BF),
     ("R16", E, F16), ("Ru", E, U16), ("L16", E, F16), ("U", E, BF), ("UR", E, F32), ("UI", E, BF), ("FR", E, F16),
     ("Rp", E, F16), ("Rpu", E, U16), ("Lu", E, U16), ("XQ", E, BF), ("o255", E, BF), ("uu", E, BF),
     ("sg1", E, BF), ("sg2", E, BF), ("qmB", E, BF), ("aa", E, F32), ("s1", E, BF), ("s2", E, BF), ("key", E, F32),
@@ -238,7 +238,7 @@ def build(rank, T, topo):
     v5, v4, ta, tc = [[tf(j, 16), tf(j + 1, 16)] for j in range(14, 22, 2)]
     qu, c5u, ju, lku, xlu, l4u = [tu(j) for j in range(6)]
     Xw, Xc, Xs, Pw, Ps = A("X", PAD, ZC + E), A("X", PAD, YC), A("X", 0, ZC), A("P", PAD, YC), A("P", 0, ZC)
-    yC, yB = A("X", YC, ZC), A("X", ZC, ZC + E)
+    yC, yB, Xd = A("X", YC, ZC), A("X", ZC, ZC + E), A("X", 0, 14336)
 
     def L(n, lo=0, hi=E):
         return A(n, lo, hi)
@@ -289,7 +289,7 @@ def build(rank, T, topo):
     ts(A("UQ", 0, 128), A("UQ", 0, 128), 0.0, ALU.is_equal)
     act(A("nIW", 0, 224), A("IW", 0, 224), ACT.Copy, scale=-1.0)
     act(A("hIW", 0, 224), A("IW", 0, 224), ACT.Copy, scale=0.5)
-    for a, v in ((nI2048, -2048.0), (I6, 6.0), (I768, 768.0), (nI768, -768.0), (I8192, 8192.0), (nI1024, -1024.0), (I2048, 2048.0)):
+    for a, v in ((nI2048, -2048.0), (I6, 6.0), (I768, 768.0), (nI768, -768.0), (I8192, 16384.0), (nI1024, -1024.0), (I2048, 4096.0)):
         act(a, I, ACT.Copy, scale=v)
     act(nSH16, SH, ACT.Copy, scale=-16.0)
     for k in range(16):
@@ -315,12 +315,18 @@ def build(rank, T, topo):
         ms(cb(4, c[0], c[1]), -16.0 if c[2] == "v" else 0.0)
     for lo in range(0, 16 * YBS, 256):
         act(A("YS", lo, lo + 256), A("r0", 0, 256), ACT.Copy, scale=0.0)
-    ms(A("MS", 0, 1248), 0.0)
-    act(A("MS", 0, 15), A("M16", 1, 16), ACT.Copy, scale=-2048.0)
+    ts(iT, A("XI", 0, 12), 16.0, ALU.mult, kcol, ALU.add)
+    ts(dN, iT, -16.0, ALU.mult, -2048.0, ALU.add)
+    ts(td, iT, -32.0, ALU.mult)
+    tt(dN, dN, td, ALU.min)
+    ms(A("MS", 0, 1280), 0.0)
+    ms(A("U5", 0, 1280), 8192.0)
+    ms(A("U4", 0, 704), 8192.0)
+    act(A("MS", 0, 15), A("M16", 1, 16), ACT.Copy, scale=A(dN[0], dN[1], dN[1] + 1))
     for b in range(1, 12):
-        act(A("MS", SEG[b] + 16 * b - 1, SEG[b + 1] - 1), A("M16", 0, 16), ACT.Copy, scale=-2048.0)
-    for b in range(12):
-        ms(A("MS", SEG[b + 1] - 1, SEG[b + 1]), 4096.0)
+        act(A("MS", SEG[b] + 16 * b - 1, SEG[b] + 16 * b + 15), A("M16", 0, 16), ACT.Copy, scale=A(dN[0], dN[1] + b, dN[1] + b + 1))
+    for b in range(11):
+        ms(A("MS", SEG[b] + 16 * b + 16, SEG[b] + 16 * b + 17), 16384.0)
     ts(c16(1), L("XI"), 512.0, ALU.add)
     ts(c16(2), L("XI"), 1552.0, ALU.add)
     ts(c16(3), L("XI"), 8.0, ALU.mult, 2048.0, ALU.add)
@@ -332,8 +338,6 @@ def build(rank, T, topo):
     cp(L("XIu"), L("XI"))
     ts(A("Dm", 0, 208), A("X16", 0, 208), kcol, ALU.is_equal)
     ts(A("Cap", 0, 208), A("Dm", 0, 208), -2048.0, ALU.mult, 2048.0, ALU.add)
-    ts(iT, A("XI", 0, 12), 16.0, ALU.mult, kcol, ALU.add)
-    ts(dN, iT, -1.0, ALU.mult, 4096.0 - YC, ALU.add)
     ts(i8, iT, 8.0, ALU.mult)
     ts(qT, iT, 8.0, ALU.mult)
     ms(qm, 0.0)
@@ -344,8 +348,8 @@ def build(rank, T, topo):
         ts(A("cT", 12 * p, 12 * p + 6), A("tf", 6 * p, 6 * p + 6), float(YC), ALU.add)
         ts(A("cT", 12 * p + 6, 12 * p + 12), A("tf", 6 * p, 6 * p + 6), 16.0, ALU.mult)
         ts(A("col", 32 + p, 33 + p), kcol, 5.0, ALU.min, 1.0 + 6 * p, ALU.add)
-        ts(A("col", 34 + p, 35 + p), A("col", 32 + p, 33 + p), 1.0, ALU.add, A("col", 32 + p, 33 + p), ALU.mult)
-        ts(A("segu", 2 * p, 2 * p + 1), A("col", 34 + p, 35 + p), 8.0, ALU.mult, -1.0 - SEG[6 * p], ALU.add)
+        ts(A("col", 34 + p, 35 + p), A("col", 32 + p, 33 + p), 1.25, ALU.add, A("col", 32 + p, 33 + p), ALU.mult)
+        ts(A("segu", 2 * p, 2 * p + 1), A("col", 34 + p, 35 + p), 8.0, ALU.mult, 4.0 * p - 3.0 - SEG[6 * p], ALU.add)
     ts(A("col", 36, 37), sbk, 64.0, ALU.add)
     ts(A("ti", 4, 5), A("col", 36, 37), 0.0, ALU.add)
     ts(A("ti", 5, 6), A("ti", 4, 5), 127, ALU.bitwise_and)
@@ -430,15 +434,18 @@ def build(rank, T, topo):
 
     def primary(t):
         ts(yC, ps(3, 0, E), MAGIC, ALU.add, -MAGIC, ALU.add)
-        act(A("YS", 0, 16 * YBS, 16), A("X", YC, YC + YBS), ACT.Copy)
         rows = [c[:2] for c in EG if c[2] != "p"]
+        y0 = rows[0][0]
+        if "s" in ONS:
+            act(A("YS", 16 * y0, 16 * YBS, 16), A("X", YC + y0, YC + YBS), ACT.Copy)
+        else:
+            ts(A("YS", 16 * y0, 16 * YBS, 16), ps(3, y0, YBS), MAGIC, ALU.add, -MAGIC, ALU.add)
         for lo, hi in rows:
             if lo >= YBS:
                 gather("s", A("YB", 16 * lo, 16 * hi), yC, L("XIu", lo, hi))
         rounded_to("y", yB, ps(4, 0, E))
-        for lo, hi in rows:
-            if lo < YBS:
-                scan(A("YB", 16 * lo, 16 * hi), A("r0", 0, 16 * (hi - lo)), A("YS", 16 * lo, 16 * hi), ALU.mult, ALU.add)
+        for lo in range(y0, YBS, 16):
+            scan(A("YB", 16 * lo, 16 * lo + 256), A("r0", 0, 256), A("YS", 16 * lo, 16 * lo + 256), ALU.mult, ALU.add)
         tt(A("ti", 0, 12), ps(5, 0, 12), orT, ALU.mult)
         ts(A("ti", 16, 28), A("ti", 0, 12), 7, ALU.bitwise_and)
         tt(qT, A("ti", 16, 28), bq, ALU.add)
@@ -510,28 +517,29 @@ def build(rank, T, topo):
     def half(a, p):
         return A(a[0], a[1] + 6 * p, a[1] + 6 * p + 6)
 
-    def first(p, since, o, u, bank, copy, val, col, sb, t0, t1, nv):
+    def first(p, since, o, u, bank, copy, val, col, sb, t0, nv):
         b0 = (96 * p - since) // 16
         at = SEG[6] * p - SEG[b0]
         top = min(since + 16 * nv, 96 * p + 96)
-        if top > 96 * p:
+        direct = "w" not in ONS
+        if top > 96 * p and not direct:
             act(L(copy, 96 * p, top), ps(bank, 96 * p, top), ACT.Copy)
         if nv < b0 + 6:
-            act(half(col, p), val, ACT.Copy, scale=-2048.0)
+            act(half(col, p), val, ACT.Copy, scale=-8192.0)
         if "b" in ONS:
-            act(A(sb[0], sb[1], sb[1] + 6), val, ACT.Copy)
+            act(A(sb[0], sb[1], sb[1] + 6), val, ACT.Copy, scale=-1.0)
         else:
-            cp(A(sb[0], sb[1], sb[1] + 6), val)
+            ts(A(sb[0], sb[1], sb[1] + 6), val, -1.0, ALU.mult)
         for b in range(b0 + 5, b0 - 1, -1):
-            j, out = b - b0, A(u, at + SEG[b], at + SEG[b + 1])
+            j, out = b - b0, A(u, at + SEG[b], at + SEG[b] + 16 * b + 16)
             if b >= nv:
-                act(out, ps(bank, since, since + 16 * b + 16), ACT.Abs, A(col[0], col[1] + 6 * p + j, col[1] + 6 * p + j + 1), 2048.0)
+                act(out, ps(bank, since, since + 16 * b + 16), ACT.Abs, A(col[0], col[1] + 6 * p + j, col[1] + 6 * p + j + 1), 8192.0)
             else:
-                ts(out, A(copy, since, since + 16 * b + 16), A(sb[0], sb[1] + j, sb[1] + j + 1), ALU.not_equal, 2048.0, ALU.mult)
-        lo, hi = at + SEG[b0], at + SEG[b0 + 6]
-        scan(A(o, lo, hi), A(u, lo, hi), A("MS", SEG[b0], SEG[b0 + 6]), ALU.min, ALU.add, 4096.0)
-        tt(t0, IND(A(o, lo, hi), A("segu", b0 // 3, b0 // 3 + 1)), sb, ALU.subtract)
-        tt(half(t1, p), A(t0[0], t0[1], t0[1] + 6), half(dN, p), ALU.max)
+                src = ps(bank, since, since + 16 * b + 16) if direct else A(copy, since, since + 16 * b + 16)
+                ts(out, src, A(val[0], val[1] + j, val[1] + j + 1), ALU.not_equal, 8192.0, ALU.mult)
+        lo, n = at + SEG[b0], SEG[b0 + 5] + 16 * b0 + 96 - SEG[b0]
+        scan(A(o, lo, lo + n), A(u, lo, lo + n), A("MS", SEG[b0], SEG[b0] + n), ALU.min, ALU.add, 8192.0)
+        tt(t0, IND(A(o, lo, lo + n), A("segu", b0 // 3, b0 // 3 + 1)), sb, ALU.min)
 
     def back(t):
         last = t == RO - 1
@@ -544,31 +552,31 @@ def build(rank, T, topo):
             tconv(ps(5, o5, o5 + 12), "WNB", A("PB", 2 * lo, 2 * hi), 192)
             mm(ps(3, lo, hi), [(ONB, c)])
             cp(half(c5u, p), ps(5, o5, o5 + 6))
-            tt(half(ncT, p), ps(5, o5 + 6, o5 + 12), half(dN, p), ALU.max)
-            act(L("oc", lo, hi), ps(2, lo, hi), ACT.Relu, 0.0, 1.0 / 4096)
+            tt(half(ncT, p), ps(5, o5 + 6, o5 + 12), half(dN, p), ALU.add)
+            act(L("oc", lo, hi), ps(2, lo, hi), ACT.Relu, 0.0, 1.0 / 8192)
             tt(L("t1", lo, hi), ps(7, lo, hi), L("oc", lo, hi), ALU.mult)
             tt(L("R16", lo, hi), ps(6, 192 + lo, 192 + hi), L("t1", lo, hi), ALU.add)
-            first(p, 0, "F5", "U5", 3, "w5", ps(5, o5, o5 + 6), b5, v5[p], ta[p], tb, n5[p])
+            first(p, 0, "F5", "U5", 3, "w5", ps(5, o5, o5 + 6), b5, v5[p], ta[p], n5[p])
+            tt(half(te, p), half(ta[p], 0), half(ncT, p), ALU.min)
             if not last:
                 cp(L("Ru", lo, hi), L("R16", lo, hi))
                 mm(ps(2, 192 + lo, 192 + hi), [(I8192, A("Dm", t + lo, t + hi)), (BK, f)])
-                act(L("A1", lo, hi), ps(2, 192 + lo, 192 + hi), ACT.Abs, 0.0, 0.375)
+                act(L("A1", lo, hi), ps(2, 192 + lo, 192 + hi), ACT.Abs, 0.0, 0.1875)
                 tt(L("m1", lo, hi), IND(Ps, half(c5u, p)), A("Cap", t + lo, t + hi), ALU.min)
                 tt(L("Lo", lo, hi), ps(7, 192 + lo, 192 + hi), L("A1", lo, hi), ALU.min)
-                ts(half(lku, p), half(tb, p), -1.0, ALU.mult, 4096.0, ALU.add)
-                tt(IND(Ps, half(lku, p)), L("m1", lo, hi), L("Lo", lo, hi), ALU.max)
+                ts(half(lku, p), half(ta[p], 0), -1.0, ALU.mult)
+                tt(IND(A("P", 0, 6160), half(lku, p)), L("m1", lo, hi), L("Lo", lo, hi), ALU.max)
         for p in range(2):
             lo, hi = VD[p]
             o4 = 384 + 16 * p
             tconv(ps(6, o4, o4 + 12), "WNn", A("PC", 2 * lo, 2 * hi), 192, [(I, A("cT", 12 * p, 12 * p + 12))])
             mm(ps(4, lo, hi), [(I, c16(2, lo, hi)), (nON, A("PC", 2 * lo, 2 * lo + 96))])
             cp(half(ju, p), ps(6, o4 + 6, o4 + 12))
-            first(p, lo, "F4", "U4", 4, "w4", ps(6, o4, o4 + 6), b4, v4[p], tc[p], td, n4[p])
-            ts(half(l4u, p), half(td, p), -1.0, ALU.mult, 4096.0, ALU.add)
-            cp(IND(Xs, half(l4u, p)), L("zero", 0, 96))
+            first(p, lo, "F4", "U4", 4, "w4", ps(6, o4, o4 + 6), b4, v4[p], tc[p], n4[p])
+            ts(half(l4u, p), half(tc[p], 0), -1.0, ALU.mult)
+            cp(IND(Xd, half(l4u, p)), L("zero", 0, 96))
         gather("s" if "e" in ONS else "v", L("evd"), A("DF", 0, 3072), ju)
-        tt(te, tb, ncT, ALU.min)
-        ts(xlu, te, -1.0, ALU.mult, 4096.0, ALU.add)
+        ts(xlu, te, -1.0, ALU.mult)
         gather("s" if "o" in ONS else "v", L("old"), Xs, c5u)
         cuts = sorted(set([0, E] + [x for c in EG if c[2] == "p" for x in c[:2]]))
         for lo, hi in zip(cuts, cuts[1:]):
@@ -576,7 +584,7 @@ def build(rank, T, topo):
             mm(ps(3, 192 + lo, 192 + hi), [(I, cb(0, lo, hi))] + ([] if whole else [(hI, A("X", ZC + lo, ZC + hi))])
                + [(hBK, L("evd", lo, hi)), (hI, L("old", lo, hi))])
         ts(L("nw"), ps(3, 192, 384), MAGIC, ALU.add, -MAGIC, ALU.add)
-        cp(IND(Xs, xlu), L("nw"))
+        cp(IND(Xd, xlu), L("nw"))
 
     for t in range(RO):
         locks(LGN if t else LG0)
@@ -642,23 +650,35 @@ def hazards(ops):
 
 
 def place(ops, pred, order, banks):
-    start, end, taken, used = {}, {}, {}, {}
+    start, end, taken = {}, {}, {}
+
+    def since(row, t):
+        j = len(row)
+        while j and row[j - 1][1] > t:
+            j -= 1
+        return j
+
     for n in order:
-        o = ops[n]
+        q, c = ops[n]["q"], ops[n]["cost"]
         t = max([end[m] + d for m, d in pred[n]] + [0.0])
-        c = o["cost"]
-        blocks = [(a, b) for a, b in taken.get(o["q"], []) if b > t]
+        row = taken.setdefault(q, [])
+        blocks = row[since(row, t):]
         for x in banks[n]:
-            blocks += [(a - GAP, b + GAP) for a, b, e in used.get(x, []) if e != o["q"] and b + GAP > t]
+            for e in "vst":
+                other = taken.get((x, e))
+                if e != q and other:
+                    blocks += [(a - GAP, b + GAP) for a, b in other[since(other, t - GAP):]]
         blocks.sort()
         for a, b in blocks:
             if t + c <= a:
                 break
-            t = max(t, b)
+            if b > t:
+                t = b
         start[n], end[n] = t, t + c
-        taken.setdefault(o["q"], []).append((t, t + c))
+        row.insert(since(row, t), (t, t + c))
         for x in banks[n]:
-            used.setdefault(x, []).append((t, t + c, o["q"]))
+            mine = taken.setdefault((x, q), [])
+            mine.insert(since(mine, t), (t, t + c))
     return start, end
 
 

from concourse.bass import DstId, RemoteDMATransfer
from concourse.mybir import AluOpType as ALU, ActivationFunctionType as ACT

N, W, E, RO = 4, 1536, 192, 4
PAD = 16
YC, ZC = PAD + W, PAD + W + E
SEG = [8 * b * (b + 1) + 2 * b + 4 * (b // 6) for b in range(12)]
MAGIC = 12582912.0
CFG = {
    "LG0": [("s", 0, 48), ("v", 96, 144), ("s", 48, 96), ("v", 144, 192)],
    "LGN": [("s", 0, 64), ("s", 64, 128), ("s", 128, 192)],
    "XG0": [("s", 0, 48), ("s", 96, 144), ("v", 48, 96), ("s", 144, 192)],
    "XGN": [("s", 0, 64), ("v", 64, 96), ("s", 96, 160), ("s", 160, 192)],
    "EG": [(0, 32, "p", 2), (32, 96, "v"), (96, 144, "v"), (144, 192, "v")],
    "VD": [(0, 96), (96, 192)],
    "YBS": 144,
    "PV": (0, 12),
    "PV4": (0, 0),
    "PVL": ((0, 0), (6, 6)),
    "ONS": "ek",
    "SUMS": [(32, 96), (96, 144), (144, 192)],
}
FOUND = {}
GAP = 240.0
CFG.update({"SEED": 1, "TURNS": 2000, "NOISE": 3000.0, "SLACK": 60.0, "SPAN": 4000.0})
CYC, GAT, SCA, PEC, HOP, VFIX, SFIX = 0.92, 1.56, 3.8, 0.46, 220.0, 15.0, 70.0

F32, F16, BF, I32, U16 = "float32", "float16", "bfloat16", "int32", "uint16"
SCRATCH = {}
for _n, _w, _d in [
    ("sti", 1728, I32), ("sth", 1728, F16), ("stx", 1728, BF), ("lah", 1728, F16), ("lax", 1728, BF),
    ("ox", 1536, BF), ("lox", 1536, BF), ("orz", 384, F32), ("lorz", 384, F32), ("zb", 192, BF),
    ("P", 6160, F32), ("X", 14336, BF), ("M8", W, BF),
    ("GL", 3072, F16), ("GX", 3072, BF), ("MX", 3072, BF), ("MN", 3072, BF),
    ("YB", 3072, BF), ("YS", 3072, BF), ("DF", 3072, BF), ("AB", 3072, BF), ("SG", 3072, BF),
    ("U5", 1280, BF), ("U4", 1280, BF), ("F5", 1280, BF), ("F4", 1280, BF), ("MS", 1280, BF),
    ("R16", E, F16), ("Ru", E, U16), ("L16", E, F16), ("U", E, BF), ("UR", E, F32), ("UI", E, BF), ("FR", E, F16),
    ("Rp", E, F16), ("Rpu", E, U16), ("Lu", E, U16), ("XQ", E, BF), ("o255", E, BF), ("uu", E, BF),
    ("sg1", E, BF), ("sg2", E, BF), ("qmB", E, BF), ("aa", E, F32), ("s1", E, BF), ("s2", E, BF), ("key", E, F32),
    ("kT", E, F32), ("mx", E, F32), ("mb", E, F32), ("oh", E, BF), ("PB", 2 * E, F16),
    ("PC", 2 * E, F16), ("oc", E, BF), ("t1", E, F32), ("A1", E, F32), ("Lo", E, F32), ("m1", E, F32),
    ("evd", E, BF), ("old", E, BF), ("nw", E, BF), ("zero", E, BF), ("rn", E, F32), ("w5", E, F16), ("w4", E, F16),
    ("tf", 352, F32), ("ti", 32, I32), ("tu", 128, U16), ("segu", 4, U16),
    ("IX", E, BF), ("XI", E, BF), ("XIu", E, U16), ("XS", 128, BF), ("UQ", 128, BF), ("VQ", 528, BF), ("X16", 208, BF),
    ("col", 64, F32), ("M16", 16, F32), ("IW", 224, BF), ("nIW", 224, BF), ("hIW", 224, BF), ("n16", 128, BF),
    ("wI", 7 * 128, BF), ("nON", 128, BF), ("ONB", 128, BF), ("TL", 128, BF), ("TLa", 128, BF),
    ("W0", 144, BF), ("WN", 144, BF), ("WN16", 144, BF), ("WNn", 144, BF), ("WNB", 144, BF),
    ("SK", 2048, BF), ("c16", 5 * E, F16), ("cb", 5 * E, BF), ("cT", 32, F16),
    ("Dm", 208, BF), ("Cap", 208, F32), ("r0", 1024, BF), ("rB", 1024, BF),
]:
    SCRATCH[_n] = ("sbuf", [128, _w], _d)
for _n in range(8):
    SCRATCH["p%d" % _n] = ("psum", [128, 512], F32)
SEMAPHORES = (["cv", "cs", "ct", "cg"] + ["d%d" % _n for _n in range(28)] + ["l%d" % _n for _n in range(8)]
              + ["%s%d" % (_k, _n) for _k in ("ah", "ax", "ao", "ar") for _n in range(N)])


def A(name, lo, hi, step=1, p0=0, p1=128):
    return (name, lo, hi, step, p0, p1)


def IND(win, off):
    return ("*", win, off)


def width(a):
    return 16 * (a[2][2] - a[2][1]) if a[0] == "*" else -(-(a[2] - a[1]) // abs(a[3]))


def narrow(*aps):
    return 0.5 if all(SCRATCH[a[0]][2] in (F16, BF, U16) for a in aps) else 1.0


def in_psum(a):
    return SCRATCH[a[0]][0] == "psum"


def build(rank, T, topo):
    ops = []
    cnt = {"d": 0, "l": 0}
    sent = {}
    LG0, LGN, XG0, XGN, EG, VD, YBS, PV, PV4 = [CFG[k] for k in ("LG0", "LGN", "XG0", "XGN", "EG", "VD", "YBS", "PV", "PV4")]

    def ap(a):
        if not isinstance(a, tuple):
            return a
        if a[0] == "*":
            return ap(a[1]).indirect(ap(a[2]))
        n, lo, hi, st, p0, p1 = a
        if st < 0:
            return T[n][p0:p1, hi - 1:(lo - 1 if lo > 0 else None):st]
        return T[n][p0:p1, lo:hi:st] if st != 1 else T[n][p0:p1, lo:hi]

    def op(q, fns, out, ins, cost, sem=None, lat=0.0, after=()):
        rd, wr = [], []
        for a in ins:
            if isinstance(a, tuple):
                rd += [a[1], a[2]] if a[0] == "*" else [a]
        if isinstance(out, tuple):
            if out[0] == "*":
                wr.append(out[1])
                rd.append(out[2])
            else:
                wr.append(out)
        ops.append({"q": q, "fn": fns, "rd": rd, "wr": wr, "sem": sem, "cost": cost, "lat": lat, "after": list(after)})

    def cost(o, i, per, fix=VFIX):
        if o[0] == "*":
            return 60 + width(o) * SCA * CYC
        if i[0] == "*":
            return 60 + width(o) * GAT * CYC
        return max(64, width(o) * per) * CYC + fix

    def rate(o, *i):
        return 1.0 if "*" in (o[0], i[0][0]) else narrow(o, *i)

    def cp(o, i):
        op("v", [lambda e: e.tensor_copy(ap(o), ap(i))], o, [i], cost(o, i, rate(o, i)))

    def tt(o, a, b, f):
        per = 1.0 if "*" in (o[0], a[0]) or in_psum(a) or in_psum(b) else 2.0
        op("v", [lambda e: e.tensor_tensor(ap(o), ap(a), ap(b), f)], o, [a, b], cost(o, a, per))

    def ts(o, a, s1, f0, s2=None, f1=None):
        if f1 is None:
            op("v", [lambda e: e.tensor_scalar(ap(o), ap(a), ap(s1), None, f0)], o, [a, s1], cost(o, a, rate(o, a)))
        else:
            op("v", [lambda e: e.tensor_scalar(ap(o), ap(a), ap(s1), ap(s2), f0, f1)], o, [a, s1, s2], cost(o, a, rate(o, a)))

    def scan(o, d0, d1, f0, f1, init=0.0):
        op("v", [lambda e: e.tensor_tensor_scan(ap(o), ap(d0), ap(d1), init, f0, f1)], o, [d0, d1], cost(o, d0, narrow(o, d0, d1)))

    def vt(o, i):
        op("v", [lambda e: e.transpose(ap(o), ap(i))], o, [i], cost(o, i, narrow(o, i)))

    def ms(o, c):
        op("v", [lambda e: e.memset(ap(o), c)], o, [], cost(o, o, narrow(o)))

    def act(o, i, f, bias=0.0, scale=1.0):
        if f == ACT.Copy:
            op("s", [lambda e: e.activation(ap(o), ap(i), f, scale=ap(scale))], o, [i, scale], cost(o, i, 1.0, SFIX))
        else:
            op("s", [lambda e: e.activation(ap(o), ap(i), f, bias=ap(bias), scale=ap(scale))], o, [i, bias, scale], cost(o, i, 1.0, SFIX))

    def mm(o, terms, start=True, stop=True):
        fns = [lambda e, l=l, r=r, j=j: e.matmul(ap(o), ap(l), ap(r), start and j == 0, stop and j == len(terms) - 1)
               for j, (l, r) in enumerate(terms)]
        op("t", fns, o, [x for lr in terms for x in lr], sum(max(min(64, width(l)), width(r)) for l, r in terms) * PEC, lat=60.0)

    def iota(o, pat, base, mult, whole=False):
        if whole:
            op("g", [lambda e: e.iota(ap(o), pat, base, mult)], o, [], 130.0)
        else:
            op("g", [lambda e: e.iota(ap(o), pat, base, mult, allow_small_or_imprecise_dtypes=True)], o, [], 130 + 2 * CYC * width(o))

    def dma(q, o, i, lat=2600.0):
        s = "d%d" % cnt["d"]
        cnt["d"] += 1
        op(q, [lambda e: e.dma_start(ap(o), ap(i))], o, [i], 100.0, (s, 16), lat)

    me = T.cores[rank]
    others = [(rank + j) % N for j in (1, 2, 3)]
    far = [d for d in others if T.cores[d] not in topo.cores_of(me)]
    near = [d for d in others if d not in far]
    NE = 4
    eng, used = {}, []
    for j, d in enumerate(far):
        es = topo.engines(me, T.cores[d])
        eng[d] = es[j * NE:(j + 1) * NE]
        used += es
    spare = [x for x in topo.engines(me, T.cores[near[0]]) if x not in used]

    def send(items):
        s = "l%d" % cnt["l"]
        cnt["l"] += 1
        srcs = [A(src, d * w, (d + 1) * w) for d, src, dst, w, kind, es in items]

        def fn(e):
            trs = []
            for (d, src, dst, w, kind, es), a in zip(items, srcs):
                rid, pid = topo.addr(T.cores[d], me)
                trs.append(RemoteDMATransfer(dst_ids=[DstId(rid=rid, pnc=pid)], dma_engine_mask=sum(1 << x for x in es),
                                             remote_sem=T.sem["%s%d" % (kind, rank)], src=ap(a),
                                             dst=ap(A(dst, rank * w, (rank + 1) * w))))
            e.remote_dma_fused(trs, local_sem=T.sem[s])
        for it in items:
            sent[(it[4], it[0] in far)] = len(ops)
        op("g", [fn], None, srcs, 1000.0, (s, -NE * len(items)), 4500.0)

    def arrive(kind, s, dst, w):
        op("a", [], A(dst, s * w, (s + 1) * w), [], 0.0, ("%s%d" % (kind, s), NE), after=[sent[(kind, s in far)]])

    def gather(q, o, win, off):
        if q == "v":
            cp(o, IND(win, off))
        else:
            act(o, IND(win, off), ACT.Copy)

    ONS = CFG["ONS"]

    def copy(name, o, i, scale=None):
        if name in ONS:
            act(o, i, ACT.Copy, scale=1.0 if scale is None else scale)
        elif scale is None:
            cp(o, i)
        else:
            ts(o, i, scale, ALU.mult)

    def rounded_to(name, o, i):
        if name in ONS:
            act(L("rn"), i, ACT.Identity, bias[MAGIC])
            act(o, L("rn"), ACT.Identity, bias[-MAGIC])
        else:
            ts(o, i, MAGIC, ALU.add, -MAGIC, ALU.add)

    I, SH, BK = A("IW", 0, 128), A("IW", 96, 224), A("IW", 32, 160)
    nI, nSH = A("nIW", 0, 128), A("nIW", 96, 224)
    hI, hSH, hBK = A("hIW", 0, 128), A("hIW", 96, 224), A("hIW", 32, 160)
    I6, I768, nI768, nI2048, I8192, nI1024, I2048 = [A("wI", 128 * j, 128 * j + 128) for j in range(7)]
    nSH16, nON, ONB, TL = A("n16", 0, 128), A("nON", 0, 128), A("ONB", 0, 128), A("TL", 0, 128)
    pcol, kcol, s16, s16p, sbk, sbkp, nk, asc, k17 = [A("col", j, j + 1) for j in range(9)]
    bias = {}
    for j, v in enumerate((-1.0, 3.0, 1.0, 255.0, -1534.5, 0.5, -2048.0, -1535.0, MAGIC, -MAGIC)):
        bias[v] = A("col", 16 + j, 17 + j)

    def c16(j, lo=0, hi=E):
        return A("c16", j * E + lo, j * E + hi)

    def cb(j, lo=0, hi=E):
        return A("cb", j * E + lo, j * E + hi)

    def tf(j, n=12):
        return A("tf", 16 * j, 16 * j + n)

    def tu(j):
        return A("tu", 16 * j, 16 * j + 12)
    iT, dN, i8, qT, qm, orT, tq, bq, b5, b4, ncT, tb, td, te = [tf(j) for j in range(14)]
    v5, v4, ta, tc = [[tf(j, 16), tf(j + 1, 16)] for j in range(14, 22, 2)]
    qu, c5u, ju, lku, xlu, l4u = [tu(j) for j in range(6)]
    Xw, Xc, Xs, Pw, Ps = A("X", PAD, ZC + E), A("X", PAD, YC), A("X", 0, ZC), A("P", PAD, YC), A("P", 0, ZC)
    yC, yB, Xd = A("X", YC, ZC), A("X", ZC, ZC + E), A("X", 0, 14336)

    def L(n, lo=0, hi=E):
        return A(n, lo, hi)

    def ps(b, lo, hi, step=1, p0=0, p1=128):
        return A("p%d" % b, lo, hi, step, p0, p1)

    def tconv(o, w, src, n, first=()):
        mm(o, list(first) + [(A(w, 16 - a, 144 - a), A(src[0], src[1] + a, src[1] + n, 16)) for a in range(16)])

    order = far + near + [rank]
    for j, d in enumerate(order):
        dma("y", A("sti", d * 432, d * 432 + 384), T.lk[32 * d:32 * d + 32, :], 2600.0 + 700 * j)
        dma("s", A("sti", d * 432 + 384, d * 432 + 432), T.rd[32 * d:32 * d + 32, :])
    for j, d in enumerate(near + far + [rank]):
        dma("y", A("stx", d * 432, d * 432 + 384), T.x0[32 * d:32 * d + 32, :], 5000.0 + 400 * j)
        dma("s", A("stx", d * 432 + 384, d * 432 + 432), T.z0[32 * d:32 * d + 32, :])
    iota(A("ti", 0, 1), [[0, 1]], 0, 1, True)
    iota(L("IX"), [[1, E]], 0, -1)
    iota(A("UQ", 0, 128), [[1, 4], [4, 32]], 0, -1)
    iota(A("XS", 0, 128), [[16, 8], [0, 16]], 0, 0)
    iota(A("X16", 0, 208), [[0, 13], [1, 16]], 0, 0)
    for d in order:
        cp(A("sth", d * 432, d * 432 + 432), A("sti", d * 432, d * 432 + 432))
    send([(d, "sth", "lah", 432, "ah", eng[d]) for d in far])
    send([(near[0], "sth", "lah", 432, "ah", spare[0::2]), (near[0], "stx", "lax", 432, "ax", spare[1::2])])
    send([(d, "stx", "lax", 432, "ax", eng[d]) for d in far])
    iota(A("M8", 0, W), [[0, E], [1, 8]], 0, 0)
    iota(A("VQ", 0, 528), [[1, 528]], -3, -4)
    for v in bias:
        ms(bias[v], v)
    cp(pcol, A("ti", 0, 1))
    ts(A("ti", 1, 2), A("ti", 0, 1), 15, ALU.bitwise_and)
    cp(kcol, A("ti", 1, 2))
    tt(s16, pcol, kcol, ALU.subtract)
    ts(s16p, s16, 16.0, ALU.add)
    ts(A("ti", 2, 3), s16, 96.0, ALU.add)
    ts(A("ti", 3, 4), A("ti", 2, 3), 127, ALU.bitwise_and)
    cp(sbk, A("ti", 3, 4))
    ts(sbkp, sbk, 16.0, ALU.add)
    ts(nk, kcol, -1.0, ALU.mult)
    ts(asc, kcol, 15.0, ALU.is_equal, 65536.0, ALU.add)
    ts(k17, kcol, -1.0, ALU.mult, 17.0, ALU.add)
    ts(A("IW", 0, 128), A("IX", 0, 128), 0.0, ALU.is_equal)
    ts(A("IW", 128, 224), A("IX", 0, 96), 0.0, ALU.is_equal)
    ts(L("XI"), L("IX"), pcol, ALU.add)
    ts(A("M16", 0, 16), A("XI", 0, 16), kcol, ALU.is_equal)
    ts(A("UQ", 0, 128), A("UQ", 0, 128), 0.0, ALU.is_equal)
    act(A("nIW", 0, 224), A("IW", 0, 224), ACT.Copy, scale=-1.0)
    act(A("hIW", 0, 224), A("IW", 0, 224), ACT.Copy, scale=0.5)
    for a, v in ((nI2048, -2048.0), (I6, 6.0), (I768, 768.0), (nI768, -768.0), (I8192, 16384.0), (nI1024, -1024.0), (I2048, 4096.0)):
        act(a, I, ACT.Copy, scale=v)
    act(nSH16, SH, ACT.Copy, scale=-16.0)
    for k in range(16):
        ts(A("SK", 128 * k, 128 * k + 128), I, A("M16", k, k + 1), ALU.mult)
    ts(nON, A("XS", 0, 128), s16, ALU.is_equal, -1.0, ALU.mult)
    ts(ONB, A("XS", 0, 128), sbk, ALU.is_equal)
    ts(A("TLa", 0, 128), A("IX", 0, 128), 0.0, ALU.is_gt, 2048.0, ALU.mult)
    tt(A("TLa", 0, 128), A("TLa", 0, 128), nON, ALU.mult)
    tt(TL, A("TLa", 0, 128), nI2048, ALU.subtract)
    ts(c16(0), L("XI"), 1728.0, ALU.add)
    ms(A("r0", 0, 1024), 1.0)
    ms(A("r0", 0, 1024, 16), 0.0)
    act(A("rB", 0, 1024), A("r0", 0, 1024), ACT.Identity, 256.0, -256.0)
    ms(A("P", 0, PAD), 0.0)
    ms(A("P", YC, ZC), 0.0)
    ms(A("X", 0, PAD), 0.0)
    ms(yC, 0.0)
    ts(A("WN", 0, 144), A("XI", 0, 144), s16p, ALU.is_equal)
    ts(A("WNB", 0, 144), A("XI", 0, 144), sbkp, ALU.is_equal)
    act(A("WN16", 0, 144), A("WN", 0, 144), ACT.Copy, scale=16.0)
    act(A("WNn", 0, 144), A("WN", 0, 144), ACT.Copy, scale=-1.0)
    for c in EG:
        ms(cb(4, c[0], c[1]), -16.0 if c[2] == "v" else 0.0)
    for lo in range(0, 16 * YBS, 256):
        act(A("YS", lo, lo + 256), A("r0", 0, 256), ACT.Copy, scale=0.0)
    ts(iT, A("XI", 0, 12), 16.0, ALU.mult, kcol, ALU.add)
    ts(dN, iT, -16.0, ALU.mult, -2048.0, ALU.add)
    ts(td, iT, -32.0, ALU.mult)
    tt(dN, dN, td, ALU.min)
    ms(A("MS", 0, 1280), 0.0)
    ms(A("U5", 0, 1280), 8192.0)
    ms(A("U4", 0, 704), 8192.0)
    act(A("MS", 0, 15), A("M16", 1, 16), ACT.Copy, scale=A(dN[0], dN[1], dN[1] + 1))
    for b in range(1, 12):
        act(A("MS", SEG[b] + 16 * b - 1, SEG[b] + 16 * b + 15), A("M16", 0, 16), ACT.Copy, scale=A(dN[0], dN[1] + b, dN[1] + b + 1))
    for b in range(11):
        ms(A("MS", SEG[b] + 16 * b + 16, SEG[b] + 16 * b + 17), 16384.0)
    ts(c16(1), L("XI"), 512.0, ALU.add)
    ts(c16(2), L("XI"), 1552.0, ALU.add)
    ts(c16(3), L("XI"), 8.0, ALU.mult, 2048.0, ALU.add)
    ms(c16(4), -767.0)
    for j, v in enumerate((-0.25, 16.0, 65536.0)):
        ms(cb(j), v)
    ts(cb(3), L("XI"), 0.0, ALU.mult, k17, ALU.add)
    ms(L("zero"), 0.0)
    cp(L("XIu"), L("XI"))
    ts(A("Dm", 0, 208), A("X16", 0, 208), kcol, ALU.is_equal)
    ts(A("Cap", 0, 208), A("Dm", 0, 208), -2048.0, ALU.mult, 2048.0, ALU.add)
    ts(i8, iT, 8.0, ALU.mult)
    ts(qT, iT, 8.0, ALU.mult)
    ms(qm, 0.0)
    cp(qu, qT)
    ms(A("tf", 224, 288), 0.0)
    ts(A("VQ", 0, 528), A("VQ", 0, 528), 0.0, ALU.is_equal)
    for p in range(2):
        ts(A("cT", 12 * p, 12 * p + 6), A("tf", 6 * p, 6 * p + 6), float(YC), ALU.add)
        ts(A("cT", 12 * p + 6, 12 * p + 12), A("tf", 6 * p, 6 * p + 6), 16.0, ALU.mult)
        ts(A("col", 32 + p, 33 + p), kcol, 5.0, ALU.min, 1.0 + 6 * p, ALU.add)
        ts(A("col", 34 + p, 35 + p), A("col", 32 + p, 33 + p), 1.25, ALU.add, A("col", 32 + p, 33 + p), ALU.mult)
        ts(A("segu", 2 * p, 2 * p + 1), A("col", 34 + p, 35 + p), 8.0, ALU.mult, 4.0 * p - 3.0 - SEG[6 * p], ALU.add)
    ts(A("col", 36, 37), sbk, 64.0, ALU.add)
    ts(A("ti", 4, 5), A("col", 36, 37), 0.0, ALU.add)
    ts(A("ti", 5, 6), A("ti", 4, 5), 127, ALU.bitwise_and)
    ts(A("col", 37, 38), A("ti", 5, 6), 16.0, ALU.add)
    ts(A("col", 38, 39), A("M16", 0, 1), 0.5, ALU.mult)
    ts(A("W0", 0, 144), A("XI", 0, 144), A("col", 37, 38), ALU.is_equal, A("col", 38, 39), ALU.mult)

    def unpack(kind, own, land, bank):
        for s in [rank] + near + far:
            if s != rank:
                arrive(kind, s, land, 432)
            src = own if s == rank else land
            h = (s + 2) % N
            for u in range(4):
                w = A("UQ", 32 * u, 32 * u + 32)
                mm(ps(bank + u, 384, 432, 1, 32 * h, 32 * h + 32), [(w, A(src, s * 432 + 384, s * 432 + 432))])
                mm(ps(bank + u, 0, 384, 1, 32 * s, 32 * s + 32), [(w, A(src, s * 432, s * 432 + 384))])
    unpack("ah", "sth", "lah", 0)
    for u in range(4):
        cp(A("Ru", 48 * u, 48 * u + 48), ps(u, 384, 432))
        cp(A("R16", 48 * u, 48 * u + 48), ps(u, 384, 432))
        if u % 2 == 0:
            act(A("P", PAD + 384 * u, PAD + 384 * u + 384), ps(u, 0, 384), ACT.Copy)
        else:
            cp(A("P", PAD + 384 * u, PAD + 384 * u + 384), ps(u, 0, 384))
    unpack("ax", "stx", "lax", 4)
    for u in range(4):
        if u % 2 == 0:
            act(A("X", PAD + 384 * u, PAD + 384 * u + 384), ps(4 + u, 0, 384), ACT.Copy)
        else:
            cp(A("X", PAD + 384 * u, PAD + 384 * u + 384), ps(4 + u, 0, 384))
        cp(A("X", ZC + 48 * u, ZC + 48 * u + 48), ps(4 + u, 384, 432))

    def locks(chunks):
        for j, (q, lo, hi) in enumerate(chunks):
            n, b, o = hi - lo, j % 3, 192 * (j // 3)
            gather(q, A("GL", 16 * lo, 16 * hi), Pw, L("Ru", lo, hi))
            mm(ps(b, o, o + n), [(A("SK", 128 * k, 128 * k + 128), A("GL", 16 * lo + k, 16 * hi, 16)) for k in range(16)])
            if "U" in ONS:
                act(L("U", lo, hi), ps(b, o, o + n), ACT.Relu, bias[-1535.0])
            else:
                ts(L("U", lo, hi), ps(b, o, o + n), float(W), ALU.is_equal)
            copy("L", L("L16", lo, hi), ps(b, o, o + n))
            mm(ps(b, o + 64, o + 64 + n), [(I, c16(0, lo, hi)), (nI, L("R16", lo, hi)), (TL, L("U", lo, hi))])
            tt(L("UR", lo, hi), L("U", lo, hi), L("R16", lo, hi), ALU.mult)
            if "F" in ONS:
                act(L("FR", lo, hi), ps(b, o + 64, o + 64 + n), ACT.Relu, bias[-2048.0])
            else:
                ts(L("FR", lo, hi), ps(b, o + 64, o + 64 + n), -2048.0, ALU.add, 0.0, ALU.max)
            mm(ps(b, o + 128, o + 128 + n), [(I, c16(0, lo, hi)), (nI2048, L("U", lo, hi)), (nON, L("FR", lo, hi))])
            tt(L("Rp", lo, hi), ps(b, o + 128, o + 128 + n), L("UR", lo, hi), ALU.max)
            cp(L("Rpu", lo, hi), L("Rp", lo, hi))

    def features(chunks):
        gather("s" if "q" in ONS else "v", L("XQ"), Xc, qu)
        tconv(ps(5, 16, 28), "WN", L("XQ"), E)
        empty = len(ops) - 1
        mm(ps(7, 192, 384), [(ONB, L("XQ"))])
        act(orT, ps(5, 16, 28), ACT.Relu, bias[1.0], -1.0)
        act(L("o255"), ps(7, 192, 384), ACT.Relu, bias[255.0], -255.0)
        tt(tq, orT, qm, ALU.mult)
        tt(bq, qT, tq, ALU.subtract)
        for (q, lo, hi) in chunks:
            n = 16 * (hi - lo)
            g, a, b = A("GX", 16 * lo, 16 * hi), A("MX", 16 * lo, 16 * hi), A("MN", 16 * lo, 16 * hi)
            gather(q, g, Xw, L("Rpu", lo, hi))
            scan(a, A("r0", 0, n), g, ALU.mult, ALU.max)
            scan(b, A("rB", 0, n), g, ALU.add, ALU.min)
        for (q, lo, hi) in chunks:
            a, b = A("MX", 16 * lo + 15, 16 * hi, 16), A("MN", 16 * lo + 15, 16 * hi, 16)
            mm(ps(3, lo, hi), [(I, cb(0, lo, hi)), (hSH, a), (hSH, b)])
            mm(ps(4, lo, hi), [(I, cb(0, lo, hi)), (hI, a), (hI, b)])
        for x in ("MX", "MN"):
            mm(ps(5, 0, 12), ([(I, cb(0, 0, 12))] if x == "MX" else [])
               + [(A("W0", 16 - a, 144 - a), A(x, 16 * a + 15, 3072, 256)) for a in range(16)], x == "MX", x == "MN")
            ops[-1]["after"].append(empty if x == "MX" else len(ops) - 4)
        mm(ps(6, 192, 384), [(nI, L("XI")), (nI2048, L("U"))])
        act(L("UI"), ps(6, 192, 384), ACT.Relu, bias[-2048.0], -1.0)
        mm(ps(2, 320, 512), [(SH, L("L16")), (SH, L("UI"))])
        mm(ps(6, 0, 192), [(SH, L("R16")), (I, cb(1))])
        cp(L("Lu"), ps(2, 320, 512))

    def primary(t):
        ts(yC, ps(3, 0, E), MAGIC, ALU.add, -MAGIC, ALU.add)
        rows = [c[:2] for c in EG if c[2] != "p"]
        y0 = rows[0][0]
        if "s" in ONS:
            act(A("YS", 16 * y0, 16 * YBS, 16), A("X", YC + y0, YC + YBS), ACT.Copy)
        else:
            ts(A("YS", 16 * y0, 16 * YBS, 16), ps(3, y0, YBS), MAGIC, ALU.add, -MAGIC, ALU.add)
        for lo, hi in rows:
            if lo >= YBS:
                gather("s", A("YB", 16 * lo, 16 * hi), yC, L("XIu", lo, hi))
        rounded_to("y", yB, ps(4, 0, E))
        for lo in range(y0, YBS, 16):
            scan(A("YB", 16 * lo, 16 * lo + 256), A("r0", 0, 256), A("YS", 16 * lo, 16 * lo + 256), ALU.mult, ALU.add)
        tt(A("ti", 0, 12), ps(5, 0, 12), orT, ALU.mult)
        ts(A("ti", 16, 28), A("ti", 0, 12), 7, ALU.bitwise_and)
        tt(qT, A("ti", 16, 28), bq, ALU.add)
        cp(qu, qT)
        cp(IND(Xc, qu), yC)
        tt(qm, qT, i8, ALU.subtract)
        mm(ps(3, 192, 384), [(I, L("o255")), (nI, yB)])
        act(L("uu"), ps(3, 192, 384), ACT.Abs)
        mm(ps(4, 192, 384), [(I, L("R16")), (I6, L("uu"))])
        mm(ps(3, 192, 384), [(I, L("L16")), (I6, L("uu"))])
        act(L("sg1"), ps(4, 192, 384), ACT.Sign, bias[-1534.5])
        act(L("sg2"), ps(3, 192, 384), ACT.Sign, bias[-1534.5])
        mm(ps(6, 192, 384), [(I, L("R16")), (I6, L("uu")), (I, c16(4)), (nI768, L("sg1"))])
        mm(ps(7, 0, 192), [(I, L("L16")), (nI, L("R16")), (I768, L("sg1")), (nI768, L("sg2"))])
        if t < RO - 1:
            gather("s", L("qmB"), A("M8", 0, W), qu)
            mm(ps(7, 192, 384), [(I, c16(3)), (nI2048, A("Dm", t, t + E)), (BK, L("qmB"))])

    def compare(lo, hi, who, how="s"):
        b = [j for j, v in enumerate(VD) if v[0] <= lo < v[1]][0]
        off, n = lo - VD[b][0], hi - lo
        d, a, s = A("DF", 16 * lo, 16 * hi), A("AB", 16 * lo, 16 * hi), A("SG", 16 * lo, 16 * hi)
        if who == "p":
            gather("s", d, A("X", PAD, ZC), L("Lu", lo, hi))
            for k in range(16):
                mm(ps(how, n * k, n * k + n), [(nI, A("X", YC + lo, YC + hi)), (I, A("DF", 16 * lo + k, 16 * hi, 16))])
            act(s, ps(how, 0, 16 * n), ACT.Sign, bias[0.5])
            act(a, ps(how, 0, 16 * n), ACT.Abs)
            mm(ps(b, off, off + n), [(nSH16, L("U", lo, hi))]
               + [(A("WN", 16 - k, 144 - k), A("SG", 16 * lo + n * k, 16 * lo + n * k + n)) for k in range(16)])
            mm(ps(b, 96 + off, 96 + off + n), [(I, cb(2, lo, hi)), (I, cb(3, lo, hi))]
               + [(A("WN16", 16 - k, 144 - k), A("AB", 16 * lo + n * k, 16 * lo + n * k + n)) for k in range(16)])
            return
        tt(d, IND(A("X", PAD, ZC), L("Lu", lo, hi)), A("YB", 16 * lo, 16 * hi), ALU.subtract)
        if who == "v":
            ts(s, d, 0.0, ALU.is_ge, 2.0, ALU.mult)
        else:
            act(s, d, ACT.Sign, bias[0.5])
        act(a, d, ACT.Abs)
        for l0, h0 in CFG["SUMS"]:
            if h0 == hi:
                off, n = l0 - VD[b][0], hi - l0
                mm(ps(b, off, off + n), [(I, cb(4, l0, hi)), (nSH16, L("U", l0, hi))]
                   + [(A("WN", 16 - k, 144 - k), A("SG", 16 * l0 + k, 16 * hi, 16)) for k in range(16)])
                mm(ps(b, 96 + off, 96 + off + n), [(I, cb(2, l0, hi)), (I, cb(3, l0, hi))]
                   + [(A("WN16", 16 - k, 144 - k), A("AB", 16 * l0 + k, 16 * hi, 16)) for k in range(16)])

    def verdict(b):
        lo, hi = VD[b]
        n = hi - lo
        sg = ps(b, 0, n)
        act(L("aa", lo, hi), sg, ACT.Abs, asc, asc)
        act(L("s2", lo, hi), sg, ACT.Sign, bias[3.0])
        act(L("s1", lo, hi), sg, ACT.Sign, bias[-1.0])
        tt(L("key", lo, hi), ps(b, 96, 96 + n), L("aa", lo, hi), ALU.min)
        mm(ps(b, 192, 192 + n), [(nSH, L("L16", lo, hi)), (nSH, L("UI", lo, hi)), (I, c16(1, lo, hi)), (nI1024, L("s2", lo, hi))])
        mm(ps(b, 288, 288 + n), [(I2048, L("s2", lo, hi)), (I2048, L("s1", lo, hi))])
        act(ps(b, 384, 384 + n), ps(b, 192, 192 + n), ACT.Relu)
        vt(L("kT", lo, hi), L("key", lo, hi))
        scan(L("mx", lo, hi), A("r0", 0, n), L("kT", lo, hi), ALU.mult, ALU.max)
        scan(A("mb", lo, hi, -1), A("r0", 0, n), A("mx", lo, hi, -1), ALU.mult, ALU.max)
        vt(ps(2, lo, hi), L("mb", lo, hi))
        tt(L("oh", lo, hi), L("key", lo, hi), ps(2, lo, hi), ALU.is_equal)
        tt(A("PB", 2 * lo, 2 * lo + n), ps(6, lo, hi), L("oh", lo, hi), ALU.mult)
        tt(A("PB", 2 * lo + n, 2 * hi), ps(b, 288, 288 + n), L("oh", lo, hi), ALU.mult)
        tt(A("PC", 2 * lo, 2 * lo + n), ps(b, 384, 384 + n), L("oh", lo, hi), ALU.mult)
        copy("k", A("PC", 2 * lo + n, 2 * hi), L("oh", lo, hi), nk)

    def half(a, p):
        return A(a[0], a[1] + 6 * p, a[1] + 6 * p + 6)

    def first(p, since, o, u, bank, copy, val, col, sb, t0, nv):
        b0 = (96 * p - since) // 16
        at = SEG[6] * p - SEG[b0]
        top = min(since + 16 * nv, 96 * p + 96)
        direct = "w" not in ONS
        if top > 96 * p and not direct:
            act(L(copy, 96 * p, top), ps(bank, 96 * p, top), ACT.Copy)
        if nv < b0 + 6:
            act(half(col, p), val, ACT.Copy, scale=-8192.0)
        if "b" in ONS:
            act(A(sb[0], sb[1], sb[1] + 6), val, ACT.Copy, scale=-1.0)
        else:
            ts(A(sb[0], sb[1], sb[1] + 6), val, -1.0, ALU.mult)
        for b in range(b0 + 5, b0 - 1, -1):
            j, out = b - b0, A(u, at + SEG[b], at + SEG[b] + 16 * b + 16)
            if b >= nv:
                act(out, ps(bank, since, since + 16 * b + 16), ACT.Abs, A(col[0], col[1] + 6 * p + j, col[1] + 6 * p + j + 1), 8192.0)
            else:
                src = ps(bank, since, since + 16 * b + 16) if direct else A(copy, since, since + 16 * b + 16)
                ts(out, src, A(val[0], val[1] + j, val[1] + j + 1), ALU.not_equal, 8192.0, ALU.mult)
        lo, n = at + SEG[b0], SEG[b0 + 5] + 16 * b0 + 96 - SEG[b0]
        scan(A(o, lo, lo + n), A(u, lo, lo + n), A("MS", SEG[b0], SEG[b0] + n), ALU.min, ALU.add, 8192.0)
        tt(t0, IND(A(o, lo, lo + n), A("segu", b0 // 3, b0 // 3 + 1)), sb, ALU.min)

    def back(t):
        last = t == RO - 1
        n5, n4 = CFG["PVL"] if last else (PV, PV4)
        for p in range(2):
            lo, hi = VD[p]
            c, f = A("PB", 2 * lo, 2 * lo + 96), A("PB", 2 * lo + 96, 2 * hi)
            o5 = 32 + 16 * p
            mm(ps(2, lo, hi), [(BK, f)])
            tconv(ps(5, o5, o5 + 12), "WNB", A("PB", 2 * lo, 2 * hi), 192)
            mm(ps(3, lo, hi), [(ONB, c)])
            cp(half(c5u, p), ps(5, o5, o5 + 6))
            tt(half(ncT, p), ps(5, o5 + 6, o5 + 12), half(dN, p), ALU.add)
            act(L("oc", lo, hi), ps(2, lo, hi), ACT.Relu, 0.0, 1.0 / 8192)
            tt(L("t1", lo, hi), ps(7, lo, hi), L("oc", lo, hi), ALU.mult)
            tt(L("R16", lo, hi), ps(6, 192 + lo, 192 + hi), L("t1", lo, hi), ALU.add)
            first(p, 0, "F5", "U5", 3, "w5", ps(5, o5, o5 + 6), b5, v5[p], ta[p], n5[p])
            tt(half(te, p), half(ta[p], 0), half(ncT, p), ALU.min)
            if not last:
                cp(L("Ru", lo, hi), L("R16", lo, hi))
                mm(ps(2, 192 + lo, 192 + hi), [(I8192, A("Dm", t + lo, t + hi)), (BK, f)])
                act(L("A1", lo, hi), ps(2, 192 + lo, 192 + hi), ACT.Abs, 0.0, 0.1875)
                tt(L("m1", lo, hi), IND(Ps, half(c5u, p)), A("Cap", t + lo, t + hi), ALU.min)
                tt(L("Lo", lo, hi), ps(7, 192 + lo, 192 + hi), L("A1", lo, hi), ALU.min)
                ts(half(lku, p), half(ta[p], 0), -1.0, ALU.mult)
                tt(IND(A("P", 0, 6160), half(lku, p)), L("m1", lo, hi), L("Lo", lo, hi), ALU.max)
        for p in range(2):
            lo, hi = VD[p]
            o4 = 384 + 16 * p
            tconv(ps(6, o4, o4 + 12), "WNn", A("PC", 2 * lo, 2 * hi), 192, [(I, A("cT", 12 * p, 12 * p + 12))])
            mm(ps(4, lo, hi), [(I, c16(2, lo, hi)), (nON, A("PC", 2 * lo, 2 * lo + 96))])
            cp(half(ju, p), ps(6, o4 + 6, o4 + 12))
            first(p, lo, "F4", "U4", 4, "w4", ps(6, o4, o4 + 6), b4, v4[p], tc[p], n4[p])
            ts(half(l4u, p), half(tc[p], 0), -1.0, ALU.mult)
            cp(IND(Xd, half(l4u, p)), L("zero", 0, 96))
        gather("s" if "e" in ONS else "v", L("evd"), A("DF", 0, 3072), ju)
        ts(xlu, te, -1.0, ALU.mult)
        gather("s" if "o" in ONS else "v", L("old"), Xs, c5u)
        cuts = sorted(set([0, E] + [x for c in EG if c[2] == "p" for x in c[:2]]))
        for lo, hi in zip(cuts, cuts[1:]):
            whole = any(c[2] == "p" and c[0] == lo for c in EG)
            mm(ps(3, 192 + lo, 192 + hi), [(I, cb(0, lo, hi))] + ([] if whole else [(hI, A("X", ZC + lo, ZC + hi))])
               + [(hBK, L("evd", lo, hi)), (hI, L("old", lo, hi))])
        ts(L("nw"), ps(3, 192, 384), MAGIC, ALU.add, -MAGIC, ALU.add)
        cp(IND(Xd, xlu), L("nw"))

    for t in range(RO):
        locks(LGN if t else LG0)
        features(XGN if t else XG0)
        primary(t)
        for c in EG:
            compare(*c)
        for b in range(len(VD)):
            verdict(b)
        back(t)

    for d in order:
        b = (d + 2) % N
        for j, src in enumerate((L("R16"), yB)):
            mm(ps(d % 2, 96 * (d // 2) + 48 * j, 96 * (d // 2) + 48 * j + 48),
               [(A("VQ", 128 * b - u + 3, 128 * b - u + 131), A(src[0], src[1] + 48 * u, src[1] + 48 * u + 48)) for u in range(4)])
    for d in range(N):
        act(A("orz", 96 * d, 96 * d + 96), ps(d % 2, 96 * (d // 2), 96 * (d // 2) + 96), ACT.Copy)
    send([(d, "orz", "lorz", 96, "ar", eng[d]) for d in far] + [(near[0], "orz", "lorz", 96, "ar", spare[0::2])])
    for j, d in enumerate(order):
        b = (0, 1, 4, 5)[j]
        mm(ps(b, 0, 384), [(A("VQ", 128 * d - u + 3, 128 * d - u + 131), A("X", PAD + 384 * u, PAD + 384 * u + 384)) for u in range(4)])
        o = A("ox", 384 * d, 384 * d + 384)
        if j % 2 == 0:
            cp(o, ps(b, 0, 384))
        else:
            act(o, ps(b, 0, 384), ACT.Copy)
        if j == len(far) - 1:
            send([(x, "ox", "lox", 384, "ao", eng[x]) for x in far])
        if j == len(far):
            send([(near[0], "ox", "lox", 384, "ao", spare[0::2])])
    for s in [rank] + near + far:
        src = "orz" if s == rank else "lorz"
        if s != rank:
            arrive("ar", s, "lorz", 96)
        dma("y", T.ro[32 * s:32 * s + 32, :], A(src, 96 * s, 96 * s + 48))
        act(A("zb", 48 * s, 48 * s + 48), A(src, 96 * s + 48, 96 * s + 96), ACT.Copy)
        dma("y", T.zo[32 * s:32 * s + 32, :], A("zb", 48 * s, 48 * s + 48))
    for j, s in enumerate([rank] + near + far):
        if s != rank:
            arrive("ao", s, "lox", 384)
        dma("s" if j % 2 == 0 else "y", T.xo[32 * s:32 * s + 32, :], A("ox" if s == rank else "lox", 384 * s, 384 * s + 384))
    return ops


def hazards(ops):
    hist, out = {}, []
    for n, o in enumerate(ops):
        deps = set()
        touch = [(a, False) for a in o["rd"]] + [(a, True) for a in o["wr"]]
        for a, w in touch:
            for (lo, hi, p0, p1, m, mw) in hist.get(a[0], []):
                if lo < a[2] and a[1] < hi and p0 < a[5] and a[4] < p1 and (w or mw):
                    deps.add(m)
        for a in o["wr"]:
            if abs(a[3]) == 1 and a[5] - a[4] == 128:
                hist[a[0]] = [h for h in hist.get(a[0], []) if not (a[1] <= h[0] and h[1] <= a[2])]
        for a, w in touch:
            hist.setdefault(a[0], []).append((a[1], a[2], a[4], a[5], n, w))
        deps.discard(n)
        out.append(deps)
    return out


def place(ops, pred, order, banks):
    start, end, taken = {}, {}, {}

    def since(row, t):
        j = len(row)
        while j and row[j - 1][1] > t:
            j -= 1
        return j

    for n in order:
        q, c = ops[n]["q"], ops[n]["cost"]
        t = max([end[m] + d for m, d in pred[n]] + [0.0])
        row = taken.setdefault(q, [])
        blocks = row[since(row, t):]
        for x in banks[n]:
            for e in "vst":
                other = taken.get((x, e))
                if e != q and other:
                    blocks += [(a - GAP, b + GAP) for a, b in other[since(other, t - GAP):]]
        blocks.sort()
        for a, b in blocks:
            if t + c <= a:
                break
            if b > t:
                t = b
        start[n], end[n] = t, t + c
        row.insert(since(row, t), (t, t + c))
        for x in banks[n]:
            mine = taken.setdefault((x, q), [])
            mine.insert(since(mine, t), (t, t + c))
    return start, end


def ranked(pred, succ, key):
    left = [len(p) for p in pred]
    free = sorted((key[n], n) for n in range(len(pred)) if not left[n])
    out = []
    while free:
        n = free.pop(0)[1]
        out.append(n)
        for m, d in succ[n]:
            left[m] -= 1
            if not left[m]:
                free.append((key[m], m))
        free.sort()
    return out


def arrange(ops):
    dep = hazards(ops)
    pred = [[] for o in ops]
    succ = [[] for o in ops]
    prev = {}
    for n, o in enumerate(ops):
        e = {m: (0.0 if ops[m]["q"] == "t" == o["q"] else ops[m]["lat"] + HOP) for m in dep[n].union(o["after"])}
        if o["q"] in "gy":
            if o["q"] in prev:
                e.setdefault(prev[o["q"]], 0.0)
            prev[o["q"]] = n
        for m, d in e.items():
            pred[n].append((m, d))
            succ[m].append((n, d))
    banks = [set(a[0] for a in o["rd"] + o["wr"] if in_psum(a)) for o in ops]
    key = [0.0] * len(ops)
    for n in range(len(ops) - 1, -1, -1):
        key[n] = min([key[m] - d for m, d in succ[n]] + [-ops[n]["lat"]]) - ops[n]["cost"]
    best, seed = None, CFG["SEED"]
    key = FOUND.get("key", key)
    for turn in range(1 if FOUND else CFG["TURNS"]):
        start, end = place(ops, pred, ranked(pred, succ, key), banks)
        span = max(end[n] + ops[n]["lat"] for n in end)
        if best is None or span < best[0]:
            best = (span, start, end)
        if span > best[0] + CFG["SLACK"]:
            end = best[2]
        back = [-end[n] for n in range(len(ops))]
        seed = (seed * 1103515245 + 12345) % 2147483648
        at = best[0] * seed / 2147483648.0
        for n in range(len(ops)):
            if abs(end[n] - at) < CFG["SPAN"]:
                seed = (seed * 1103515245 + 12345) % 2147483648
                back[n] += CFG["NOISE"] * (seed / 2147483648.0 - 0.5)
        s2, e2 = place(ops, succ, ranked(succ, pred, back), banks)
        key = [-e2[n] for n in range(len(ops))]
    FOUND.setdefault("key", [best[1][n] for n in range(len(ops))])
    FOUND["span"] = best[0]
    return [ops[n] for n in sorted(range(len(ops)), key=lambda n: (best[1][n], n))]


def waits_of(ops):
    dep = hazards(ops)
    bank, known, clock, need = {}, {}, [], []
    for n, o in enumerate(ops):
        q = o["q"]
        deps = set(m for m in dep[n] if q != "t" or ops[m]["q"] != "t")
        for a in o["rd"] + o["wr"]:
            if in_psum(a):
                deps.update(m for e, m in bank.get(a[0], {}).items() if e != q)
                bank.setdefault(a[0], {})[q] = n
        kn = known.setdefault(q, {})
        ws = []
        for m in sorted(deps, reverse=True):
            key = ops[m]["q"] if ops[m]["sem"] is None else ops[m]["sem"][0]
            if kn.get(key, -1) < m:
                ws.append(m)
                for k, v in clock[m].items():
                    kn[k] = max(kn.get(k, -1), v)
                kn[key] = m
        clock.append(dict(kn) if q != "a" else {})
        need.append(ws if q != "a" else [])
    return need


def rank_program(g, core, T, topo):
    rank = T.rank_of(core)
    if rank is None:
        return
    ops = arrange(build(rank, T, topo))
    need = waits_of(ops)
    queue = {"v": g.vector, "s": g.scalar, "t": g.tensor, "g": g, "y": g.sync}
    waited = set(m for ws in need for m in ws)
    count, at = {}, {}
    for n, o in enumerate(ops):
        q, sem = o["q"], o["sem"]
        for m in need[n]:
            queue[q].wait_ge(T.sem[at[m][0]], at[m][1])
        ins = None
        for fn in o["fn"]:
            ins = fn(queue[q])
        if sem is not None:
            at[n] = (sem[0], abs(sem[1]))
            if q != "a" and sem[1] > 0:
                ins.then_inc(T.sem[sem[0]], 16)
        elif n in waited:
            count[q] = count.get(q, 0) + 1
            at[n] = ("c" + q, count[q])
            ins.then_inc(T.sem["c" + q], 1)
    for n, o in enumerate(ops):
        if o["sem"] is not None and n not in waited:
            g.sync.wait_ge(T.sem[at[n][0]], at[n][1])
